import numpy as np
import ml_dtypes


def mxq(x, axis, fmt="e4m3"):
    dtype, down = {"e4m3": (ml_dtypes.float8_e4m3fn, 7), "e5m2": (ml_dtypes.float8_e5m2, 14)}[fmt]
    v = np.moveaxis(np.asarray(x, np.float32).astype(ml_dtypes.bfloat16).astype(np.float64), axis, -1)
    blocks = v.reshape(v.shape[:-1] + (-1, 32))
    amax = np.abs(blocks).max(-1, keepdims=True)
    byte = np.maximum(np.where(amax > 0, np.frexp(amax)[1] - 1 + 127, 0) - down, 1)
    scale = np.exp2(byte - 127.0)
    codes = (blocks / scale).astype(np.float32).astype(dtype).astype(np.float64)
    return np.moveaxis((codes * scale).reshape(v.shape), -1, axis)


WIDE = False


def mx_kscale(k):
    if not WIDE:
        return np.ones(k)
    levels = np.array([10, -10, 5, -5, 0])
    if k % 512:
        return np.exp2(np.random.permutation(np.resize(levels, k // 32))).repeat(32)
    a = np.empty((k // 512, 16))
    for p in range(k // 512):
        a[p, :8] = np.random.permutation(np.resize(levels, 8))
        for g in range(8):
            far = levels[np.abs(levels - a[p, g]) >= 10]
            a[p, g + 8] = far[np.random.randint(len(far))]
    return np.exp2(a.ravel()).repeat(32)


def f64(x):
    return np.asarray(x).astype(np.float64)


def striped(idx):
    return np.tile(idx.reshape(-1, 16).T, (8, 1)).astype(np.uint16)


def unstriped(offs):
    return offs[:16].T.reshape(-1).astype(np.int64)


E2M1 = np.array([0.0, 0.5, 1.0, 1.5, 2.0, 3.0, 4.0, 6.0, -0.0, -0.5, -1.0, -1.5, -2.0, -3.0, -4.0, -6.0])


def pack_weight(w, fmt):
    k, n = w.shape
    w = f64(np.asarray(w, np.float32).astype(ml_dtypes.bfloat16)).reshape(k // 32, 32, n)
    amax = np.abs(w).max(1)
    if fmt == "e4m3":
        byte = np.frexp(amax)[1] - 1 + 127 - 7
    else:
        mant, ex = np.frexp(amax / 6.0)
        byte = np.where(mant > 0.5, ex, ex - 1) + 127
    byte = np.clip(np.where(amax > 0, byte, 1), 1, 254)
    scaled = (w * np.exp2(127.0 - byte)[:, None, :]).reshape(k, n).astype(np.float32)
    by_word = np.ascontiguousarray(scaled.reshape(k // 512, 128, 4, n).transpose(0, 1, 3, 2))
    if fmt == "e4m3":
        words = by_word.astype(ml_dtypes.float8_e4m3fn).view(np.uint8)
    else:
        c = by_word.astype(ml_dtypes.float4_e2m1fn).view(np.uint8) & 0xF
        words = (c[..., 0::2] | (c[..., 1::2] << 4)).reshape(k // 512, 128, 2 * n)
    return np.ascontiguousarray(words), np.ascontiguousarray(byte.astype(np.uint8).reshape(k // 512, 16, n))


def unpack_weight(words, scales, fmt):
    g, _, n = scales.shape
    words = np.ascontiguousarray(words).reshape(g, 128, n, -1)
    if fmt == "e4m3":
        vals = words.view(ml_dtypes.float8_e4m3fn).astype(np.float64)
    else:
        nib = np.empty((g, 128, n, 4), np.uint8)
        nib[..., 0::2] = words & 0xF
        nib[..., 1::2] = words >> 4
        vals = E2M1[nib]
    vals = vals * np.repeat(np.exp2(scales.astype(np.float64) - 127.0), 8, axis=1)[..., None]
    return vals.transpose(0, 1, 3, 2).reshape(g * 512, n)


def silu(v):
    return v / (1.0 + np.exp(-np.maximum(v, -700.0)))


K, T, E, C, H, N = 512, 512, 8, 128, 512, 512


def by_expert(wq, xq):
    return np.concatenate([wq[e].T @ xq[:, e * C:(e + 1) * C] for e in range(E)], axis=1)


def setup_inputs():
    n = np.random.standard_normal
    s = mx_kscale(K)
    u = mx_kscale(H)
    first = np.random.permutation(np.repeat(np.arange(E), T // E))
    second = (first + 1 + np.random.permutation(np.repeat(np.arange(E - 1), -(-T // (E - 1)))[:T])) % E
    while np.bincount(second, minlength=E).max() != T // E:
        load = np.bincount(second, minlength=E); hi, lo = int(load.argmax()), int(load.argmin())
        t = np.flatnonzero((second == hi) & (first != lo))[0]; second[t] = lo
    slot_token = np.empty(E * C, np.int64); pos = np.empty((2, T), np.int64); fill = np.zeros(E, np.int64)
    place = np.stack([np.random.permutation(C) for _ in range(E)])
    for r, deal in enumerate((first, second)):
        for t in np.random.permutation(T):
            e = deal[t]; j = e * C + place[e, fill[e]]; fill[e] += 1; slot_token[j] = t; pos[r, t] = j
    g = np.random.uniform(0.2, 0.8, T)
    x = pack_weight(n((K, T)) * s[:, None], "e4m3")
    w2 = pack_weight(n((H, N)) / np.sqrt(H) / u[:, None], "e4m3")
    return {
        "x_words": x[0],
        "x_scales": x[1],
        "w1": (n((E, K, H)) / np.sqrt(K) / s[None, :, None]).astype(np.float32),
        "w3": (n((E, K, H)) / np.sqrt(K) / s[None, :, None] * u).astype(np.float32),
        "w2_words": w2[0],
        "w2_scales": w2[1],
        "gate": np.stack([np.tile(g, (128, 1)), np.tile(1.0 - g, (128, 1))]).astype(np.float32),
        "offs": striped(slot_token),
        "pos1": striped(pos[0]),
        "pos2": striped(pos[1]),
    }


def reference(x_words, x_scales, w1, w3, w2_words, w2_scales, gate, offs, pos1, pos2):
    w1q = mxq(f64(w1), 1, "e4m3")
    w3q = mxq(f64(w3), 1, "e4m3")
    w2 = unpack_weight(w2_words, w2_scales, "e4m3")
    idx = unstriped(offs)
    xq = unpack_weight(x_words, x_scales, "e4m3")[:, idx]
    h = silu(by_expert(w1q, xq)) * by_expert(w3q, xq)
    c = sum(f64(gate[r, :1]) * h[:, unstriped(p)] for r, p in enumerate((pos1, pos2)))
    return w2.T @ mxq(c, 0, "e4m3")

@@ -1,0 +1,242 @@
+from contextlib import ExitStack
+
+import concourse.mybir as mybir
+from concourse.masks import make_identity
+
+K, T, E, C, H, N = 512, 512, 8, 128, 512, 512
+S = E * C
+FLOPS = 2 * 2 * K * H * S + 2 * H * N * T
+
+F32 = mybir.dt.float32
+BF16 = mybir.dt.bfloat16
+I32 = mybir.dt.int32
+U32 = mybir.dt.uint32
+U16 = mybir.dt.uint16
+U8 = mybir.dt.uint8
+FP8X4 = mybir.dt.float8_e4m3fn_x4
+SILU = mybir.ActivationFunctionType.Silu
+MULT = mybir.AluOpType.mult
+
+P = 128
+PACK = 4
+CH = H // P
+TB = T // P
+SPLIT = 2
+XG = 256
+
+
+def tile_moe_sdn_glu_silu_kernel(
+    tc, x_words, x_scales, w1, w3, w2_words, w2_scales, gate, offs, pos1, pos2, out
+):
+    nc = tc.nc
+    whole = E - SPLIT
+    with ExitStack() as ctx:
+        keep = ctx.enter_context(tc.tile_pool(name="keep", bufs=1))
+        ring = ctx.enter_context(tc.tile_pool(name="ring", bufs=3))
+        psum = ctx.enter_context(tc.psum_pool(name="psum", bufs=1))
+        bank = [psum.tile([P, 512], F32, name=f"bank{i}") for i in range(8)]
+
+        offs_sb = keep.tile([P, S // 16], U16, name="offs_sb")
+        pos_sb = [keep.tile([P, T // 16], U16, name=f"pos_sb{r}") for r in range(2)]
+        xw = keep.tile([P, T], I32, name="xw", align_bytes=64)
+        xs = keep.tile([P, T], U8, name="xs", align_bytes=64)
+        w2w = keep.tile([P, N], I32, name="w2w", align_bytes=64)
+        w2s = keep.tile([P, N], U8, name="w2s", align_bytes=64)
+        xgw = keep.tile([P, S], U32, name="xgw", align_bytes=64)
+        xgs = keep.tile([P, S], U8, name="xgs", align_bytes=64)
+        gate_sb = keep.tile([P, 2, T], F32, name="gate_sb")
+        ident = keep.tile([P, P], F32, name="ident")
+        warm = keep.tile([P, 8], F32, name="warm")
+        h = [keep.tile([P, S], F32, name=f"h{q}") for q in range(CH)]
+        cb = keep.tile([P, TB, H], BF16, name="cb", align_bytes=64)
+
+        nc.vector.memset(xs[:].bitcast(I32), 0)
+        nc.vector.memset(warm[:], 0.0)
+        nc.vector.memset(w2s[:].bitcast(I32), 0)
+        make_identity(nc, ident[:])
+
+        def load_scales(engine, plane, rows):
+            for g in range(4):
+                engine.dma_start(
+                    out=plane[32 * g : 32 * g + 4, :].bitcast(I32),
+                    in_=rows[4 * g : 4 * g + 4, :].bitcast(I32),
+                )
+
+        def load_words(tile, words):
+            nc.sync.dma_start(out=tile[:], in_=words.rearrange("p t d -> p (t d)").bitcast(I32))
+
+        raw = {}
+
+        def load_piece(m, e, c0, width):
+            src = (w1, w3)[m]
+            t = keep.tile([P, PACK, width], F32, name=f"raw{m}_{e}_{c0}")
+            nc.sync.dma_start(
+                out=t[:], in_=src[e].rearrange("(p j) c -> p j c", j=PACK)[:, :, c0 : c0 + width]
+            )
+            raw[(m, e, c0)] = t
+
+        nc.sync.dma_start(offs_sb[:], offs)
+        load_words(xw, x_words[0])
+        load_scales(nc.scalar, xs, x_scales[0])
+        nc.scalar.activation(warm[:], warm[:], SILU)
+        load_piece(0, 0, 0, H)
+        load_piece(1, 0, 0, H)
+        for e in range(1, whole):
+            load_piece(0, e, 0, H)
+            load_piece(1, e, 0, H)
+        nc.sync.dma_start(pos_sb[0][:], pos1)
+        nc.sync.dma_start(pos_sb[1][:], pos2)
+        nc.sync.dma_start(gate_sb[:], gate.rearrange("r p t -> p r t"))
+        for q in range(CH):
+            for m in range(2):
+                for e in range(whole, E):
+                    load_piece(m, e, q * P, P)
+        load_words(w2w, w2_words[0])
+        load_scales(nc.sync, w2s, w2_scales[0])
+
+        def gather_tokens(a):
+            sl = offs_sb[:, a // 16 : (a + XG) // 16]
+            nc.vector.tensor_copy(xgw[:, a : a + XG], xw[:].bitcast(U32).indirect(sl))
+            nc.vector.tensor_copy(xgs[:, a : a + XG], xs[:].indirect(sl))
+
+        def flat(m, e, c0):
+            return raw[(m, e, c0)][:].rearrange("p j c -> p (j c)")
+
+        def quantize(g, width):
+            codes = ring.tile([P, width], U32, name="codes", tag=f"codes{width}", align_bytes=64, bufs=4)
+            scales = ring.tile([P, width], U8, name="scales", tag=f"scales{width}", align_bytes=64, bufs=4)
+            nc.vector.quantize_mx(
+                out=codes[:].bitcast(FP8X4), scales=scales[:], in_=g[:].rearrange("p c j -> p (c j)")
+            )
+            return codes, scales
+
+        def piece(engine, m, e, c0, width, acc):
+            g = ring.tile([P, width, PACK], BF16, name="grouped", tag=f"grouped{width}", align_bytes=64, bufs=4)
+            dst = g[:].rearrange("p (c i) j -> p c j i", i=4)
+            src = raw[(m, e, c0)][:].rearrange("p j (c i) -> p c j i", i=4)
+            if engine == "v":
+                nc.vector.tensor_copy(dst, src)
+            else:
+                nc.scalar.copy(dst, src)
+            codes, scales = quantize(g, width)
+            for a in range(0, width, P):
+                nc.tensor.matmul_mx(
+                    out=acc[:, a : a + C],
+                    lhsT=codes[:, a : a + P].bitcast(FP8X4),
+                    lhsT_scale=scales[:, a : a + P],
+                    rhs=xgw[:, e * C : (e + 1) * C].bitcast(FP8X4),
+                    rhs_scale=xgs[:, e * C : (e + 1) * C],
+                    start=True,
+                    stop=True,
+                )
+
+        def gate_whole(e, sa):
+            nc.scalar.activation(sa, bank[e % 2][:], SILU)
+            for q in range(CH):
+                cols = slice(q * C, (q + 1) * C)
+                nc.vector.tensor_tensor(h[q][:, e * C : (e + 1) * C], bank[2 + e % 2][:, cols], sa[:, cols], MULT)
+
+        def weigh(q, t0, width, dst):
+            for r in range(2):
+                sl = pos_sb[r][:, t0 // 16 : (t0 + width) // 16]
+                nc.vector.tensor_tensor(
+                    dst[:, r * width : (r + 1) * width], h[q][:].indirect(sl), gate_sb[:, r, t0 : t0 + width], MULT
+                )
+
+        def turn(src, width, ct):
+            for a in range(0, width, P):
+                for r in range(2):
+                    nc.tensor.matmul(
+                        ct[:, a : a + P],
+                        lhsT=src[:, r * width + a : r * width + a + P],
+                        rhs=ident[:],
+                        is_transpose=True,
+                        start=(r == 0),
+                        stop=(r == 1),
+                    )
+
+        half = T // 2
+
+        def turn_chunk(q, ct):
+            turn(flat(0, E - 1, (q + 1) * P), half, ct[:, 0:half])
+            turn(flat(1, E - 1, (q + 1) * P), half, ct[:, half:T])
+            nc.scalar.copy(cb[:, :, q * P : (q + 1) * P], ct[:].rearrange("p (b c) -> p b c", c=P))
+
+        def split_chunk(q):
+            k = whole + q
+            a, b = bank[k % 2], bank[2 + k % 2]
+            for u in range(SPLIT):
+                piece("s", 0, whole + u, q * P, P, a[:, u * C : (u + 1) * C])
+                if q == 0 and u == 0:
+                    gate_whole(whole - 1, flat(0, whole, 0))
+            if q > 0:
+                weigh(q - 1, 0, half, flat(0, E - 1, q * P))
+            for u in range(SPLIT):
+                piece("v" if q == 0 else "s", 1, whole + u, q * P, P, b[:, u * C : (u + 1) * C])
+            sa = flat(1, whole, q * P)[:, 0 : SPLIT * C]
+            nc.scalar.activation(sa, a[:, 0 : SPLIT * C], SILU)
+            if q > 0:
+                weigh(q - 1, half, half, flat(1, E - 1, q * P))
+            nc.vector.tensor_tensor(h[q][:, whole * C :], b[:, 0 : SPLIT * C], sa, MULT)
+            if q > 1:
+                turn_chunk(q - 2, a)
+
+        def last_chunk(b):
+            u = ring.tile([P, 2 * P], F32, name="u", tag="u", bufs=4)
+            weigh(CH - 1, b * P, P, u[:])
+            ct = bank[5 - b % 2][:, 0:P]
+            turn(u[:], P, ct)
+            nc.scalar.copy(cb[:, b, (CH - 1) * P :], ct)
+
+        def finish(b):
+            words = cb[:, b, :].bitcast(F32)
+            xt = bank[6 + b % 2][:, 0 : 2 * P].rearrange("p (u t) -> p u t", u=2)
+            for u in range(2):
+                nc.tensor.transpose(xt[:, u, :], words[:, u : H // 2 : 2], ident[:])
+            g = ring.tile([P, P, PACK], BF16, name="cg", tag="cg", align_bytes=64, bufs=4)
+            nc.scalar.copy(
+                g[:].rearrange("p t j -> p (t j)").bitcast(F32).rearrange("p (t u) -> p t u", u=2),
+                xt.rearrange("p u t -> p t u"),
+            )
+            codes, scales = quantize(g, P)
+            for k in range(2):
+                o = bank[2 * (b % 2) + k]
+                for c in range(2):
+                    n0 = (2 * k + c) * P
+                    nc.tensor.matmul_mx(
+                        out=o[:, c * P : (c + 1) * P],
+                        lhsT=w2w[:, n0 : n0 + P].bitcast(FP8X4),
+                        lhsT_scale=w2s[:, n0 : n0 + P],
+                        rhs=codes[:].bitcast(FP8X4),
+                        rhs_scale=scales[:],
+                        start=True,
+                        stop=True,
+                    )
+                res = ring.tile([P, 2, P], F32, name="res", tag="res", bufs=8)
+                src = o[:, 0 : 2 * P].rearrange("p (c t) -> p c t", c=2)
+                if k == 0:
+                    nc.scalar.copy(res[:], src)
+                else:
+                    nc.vector.tensor_copy(res[:], src)
+                nc.sync.dma_start(
+                    out=out.rearrange("(c p) t -> p c t", p=P)[:, 2 * k : 2 * k + 2, b * P : (b + 1) * P],
+                    in_=res[:],
+                )
+
+        for e in range(whole):
+            if e * C % XG == 0:
+                gather_tokens(e * C)
+            piece("s", 0, e, 0, H, bank[e % 2])
+            if e > 0:
+                gate_whole(e - 1, flat(0, e, 0)[:, 0:H])
+            piece("v", 1, e, 0, H, bank[2 + e % 2])
+        for a in range(-(-whole * C // XG) * XG, S, XG):
+            gather_tokens(a)
+        for q in range(CH):
+            split_chunk(q)
+        turn_chunk(CH - 2, bank[4])
+        for b in range(TB):
+            last_chunk(b)
+            if b > 0:
+                finish(b - 1)
+        finish(TB - 1)

@@ -21,8 +21,11 @@ P = 128
 PACK = 4
 CH = H // P
 TB = T // P
-SPLIT = 2
+SPLIT = 3
 XG = 256
+W3_SCALAR_COLS = 128
+FIRST_VECTOR_COLS = 256
+LATER_VECTOR_COLS = 0
 
 
 def tile_moe_sdn_glu_silu_kernel(
@@ -30,9 +33,11 @@ def tile_moe_sdn_glu_silu_kernel(
 ):
     nc = tc.nc
     whole = E - SPLIT
+    wide = SPLIT * P
+    half = T // 2
     with ExitStack() as ctx:
         keep = ctx.enter_context(tc.tile_pool(name="keep", bufs=1))
-        ring = ctx.enter_context(tc.tile_pool(name="ring", bufs=3))
+        ring = ctx.enter_context(tc.tile_pool(name="ring", bufs=4))
         psum = ctx.enter_context(tc.psum_pool(name="psum", bufs=1))
         bank = [psum.tile([P, 512], F32, name=f"bank{i}") for i in range(8)]
 
@@ -49,6 +54,8 @@ def tile_moe_sdn_glu_silu_kernel(
         warm = keep.tile([P, 8], F32, name="warm")
         h = [keep.tile([P, S], F32, name=f"h{q}") for q in range(CH)]
         cb = keep.tile([P, TB, H], BF16, name="cb", align_bytes=64)
+        raw_whole = [[keep.tile([P, PACK, H], F32, name=f"raw{m}_{e}") for e in range(whole)] for m in range(2)]
+        raw_chunk = [[keep.tile([P, PACK, wide], F32, name=f"rawc{m}_{q}") for q in range(CH)] for m in range(2)]
 
         nc.vector.memset(xs[:].bitcast(I32), 0)
         nc.vector.memset(warm[:], 0.0)
@@ -65,32 +72,32 @@ def tile_moe_sdn_glu_silu_kernel(
         def load_words(tile, words):
             nc.sync.dma_start(out=tile[:], in_=words.rearrange("p t d -> p (t d)").bitcast(I32))
 
-        raw = {}
+        def rows_of(m, e):
+            return (w1, w3)[m][e].rearrange("(p j) c -> p j c", j=PACK)
 
-        def load_piece(m, e, c0, width):
-            src = (w1, w3)[m]
-            t = keep.tile([P, PACK, width], F32, name=f"raw{m}_{e}_{c0}")
-            nc.sync.dma_start(
-                out=t[:], in_=src[e].rearrange("(p j) c -> p j c", j=PACK)[:, :, c0 : c0 + width]
-            )
-            raw[(m, e, c0)] = t
+        def load_chunk(m, q):
+            for u in range(SPLIT):
+                nc.sync.dma_start(
+                    out=raw_chunk[m][q][:, :, u * P : (u + 1) * P],
+                    in_=rows_of(m, whole + u)[:, :, q * P : (q + 1) * P],
+                )
 
         nc.sync.dma_start(offs_sb[:], offs)
         load_words(xw, x_words[0])
         load_scales(nc.scalar, xs, x_scales[0])
         nc.scalar.activation(warm[:], warm[:], SILU)
-        load_piece(0, 0, 0, H)
-        load_piece(1, 0, 0, H)
-        for e in range(1, whole):
-            load_piece(0, e, 0, H)
-            load_piece(1, e, 0, H)
+        for e in range(whole):
+            for m in range(2):
+                nc.sync.dma_start(out=raw_whole[m][e][:], in_=rows_of(m, e))
         nc.sync.dma_start(pos_sb[0][:], pos1)
         nc.sync.dma_start(pos_sb[1][:], pos2)
-        nc.sync.dma_start(gate_sb[:], gate.rearrange("r p t -> p r t"))
+        gate_rows = gate.rearrange("r p t -> p r t")
         for q in range(CH):
             for m in range(2):
-                for e in range(whole, E):
-                    load_piece(m, e, q * P, P)
+                load_chunk(m, q)
+                if q == 1:
+                    cols = slice(m * half, (m + 1) * half)
+                    nc.sync.dma_start(gate_sb[:, :, cols], gate_rows[:, :, cols])
         load_words(w2w, w2_words[0])
         load_scales(nc.sync, w2s, w2_scales[0])
 
@@ -99,42 +106,48 @@ def tile_moe_sdn_glu_silu_kernel(
             nc.vector.tensor_copy(xgw[:, a : a + XG], xw[:].bitcast(U32).indirect(sl))
             nc.vector.tensor_copy(xgs[:, a : a + XG], xs[:].indirect(sl))
 
-        def flat(m, e, c0):
-            return raw[(m, e, c0)][:].rearrange("p j c -> p (j c)")
+        def flat(tile):
+            return tile[:].rearrange("p j c -> p (j c)")
 
         def quantize(g, width):
-            codes = ring.tile([P, width], U32, name="codes", tag=f"codes{width}", align_bytes=64, bufs=4)
-            scales = ring.tile([P, width], U8, name="scales", tag=f"scales{width}", align_bytes=64, bufs=4)
-            nc.vector.quantize_mx(
-                out=codes[:].bitcast(FP8X4), scales=scales[:], in_=g[:].rearrange("p c j -> p (c j)")
-            )
+            codes = ring.tile([P, width], U32, name="codes", tag=f"codes{width}", align_bytes=64)
+            scales = ring.tile([P, width], U8, name="scales", tag=f"scales{width}", align_bytes=64)
+            for a, b in ([(0, 256), (256, 384)] if width == 384 else [(0, width)]):
+                nc.vector.quantize_mx(
+                    out=codes[:, a:b].bitcast(FP8X4),
+                    scales=scales[:, a:b],
+                    in_=g[:, a:b, :].rearrange("p c j -> p (c j)"),
+                )
             return codes, scales
 
-        def piece(engine, m, e, c0, width, acc):
-            g = ring.tile([P, width, PACK], BF16, name="grouped", tag=f"grouped{width}", align_bytes=64, bufs=4)
-            dst = g[:].rearrange("p (c i) j -> p c j i", i=4)
-            src = raw[(m, e, c0)][:].rearrange("p j (c i) -> p c j i", i=4)
-            if engine == "v":
-                nc.vector.tensor_copy(dst, src)
-            else:
-                nc.scalar.copy(dst, src)
+        def multiply(raw, width, scalar_cols, experts, acc, g=None):
+            if g is None:
+                g = ring.tile([P, width, PACK], BF16, name="grouped", tag=f"grouped{width}", align_bytes=64)
+            for a, b, copy in ((0, scalar_cols, nc.scalar.copy), (scalar_cols, width, nc.vector.tensor_copy)):
+                if b > a:
+                    copy(
+                        g[:, a:b, :].rearrange("p (c i) j -> p c j i", i=4),
+                        raw[:, :, a:b].rearrange("p j (c i) -> p c j i", i=4),
+                    )
             codes, scales = quantize(g, width)
-            for a in range(0, width, P):
+            for k, e in enumerate(experts):
+                cols = slice(k * P, (k + 1) * P)
                 nc.tensor.matmul_mx(
-                    out=acc[:, a : a + C],
-                    lhsT=codes[:, a : a + P].bitcast(FP8X4),
-                    lhsT_scale=scales[:, a : a + P],
+                    out=acc[:, cols],
+                    lhsT=codes[:, cols].bitcast(FP8X4),
+                    lhsT_scale=scales[:, cols],
                     rhs=xgw[:, e * C : (e + 1) * C].bitcast(FP8X4),
                     rhs_scale=xgs[:, e * C : (e + 1) * C],
                     start=True,
                     stop=True,
                 )
 
-        def gate_whole(e, sa):
-            nc.scalar.activation(sa, bank[e % 2][:], SILU)
+        def gate_whole(e, landing):
+            sa = landing[:, :, 0:C]
+            nc.scalar.activation(sa, bank[e % 2][:].rearrange("p (q c) -> p q c", c=C), SILU)
             for q in range(CH):
                 cols = slice(q * C, (q + 1) * C)
-                nc.vector.tensor_tensor(h[q][:, e * C : (e + 1) * C], bank[2 + e % 2][:, cols], sa[:, cols], MULT)
+                nc.vector.tensor_tensor(h[q][:, e * C : (e + 1) * C], bank[2 + e % 2][:, cols], sa[:, q, :], MULT)
 
         def weigh(q, t0, width, dst):
             for r in range(2):
@@ -155,88 +168,92 @@ def tile_moe_sdn_glu_silu_kernel(
                         stop=(r == 1),
                     )
 
-        half = T // 2
-
-        def turn_chunk(q, ct):
-            turn(flat(0, E - 1, (q + 1) * P), half, ct[:, 0:half])
-            turn(flat(1, E - 1, (q + 1) * P), half, ct[:, half:T])
-            nc.scalar.copy(cb[:, :, q * P : (q + 1) * P], ct[:].rearrange("p (b c) -> p b c", c=P))
 
         def split_chunk(q):
             k = whole + q
             a, b = bank[k % 2], bank[2 + k % 2]
-            for u in range(SPLIT):
-                piece("s", 0, whole + u, q * P, P, a[:, u * C : (u + 1) * C])
-                if q == 0 and u == 0:
-                    gate_whole(whole - 1, flat(0, whole, 0))
+            experts = range(whole, E)
+            multiply(raw_chunk[0][q], wide, wide, experts, a)
             if q > 0:
-                weigh(q - 1, 0, half, flat(0, E - 1, q * P))
-            for u in range(SPLIT):
-                piece("v" if q == 0 else "s", 1, whole + u, q * P, P, b[:, u * C : (u + 1) * C])
-            sa = flat(1, whole, q * P)[:, 0 : SPLIT * C]
-            nc.scalar.activation(sa, a[:, 0 : SPLIT * C], SILU)
+                weigh(q - 1, 0, half, flat(raw_chunk[0][q]))
+                turn(flat(raw_chunk[0][q]), half, bank[3 + q][:, 0:half])
+            g = None
+            if q == CH - 1:
+                g = cb[:].rearrange("p b i -> p (b i)")[:, 0 : wide * PACK].rearrange("p (c j) -> p c j", j=PACK)
+            multiply(raw_chunk[1][q], wide, wide - (LATER_VECTOR_COLS if q else FIRST_VECTOR_COLS), experts, b, g)
+            sa = flat(raw_chunk[1][q])[:, T : T + wide]
+            nc.scalar.activation(sa, a[:, 0:wide], SILU)
             if q > 0:
-                weigh(q - 1, half, half, flat(1, E - 1, q * P))
-            nc.vector.tensor_tensor(h[q][:, whole * C :], b[:, 0 : SPLIT * C], sa, MULT)
-            if q > 1:
-                turn_chunk(q - 2, a)
+                weigh(q - 1, half, half, flat(raw_chunk[1][q]))
+            nc.vector.tensor_tensor(h[q][:, whole * C :], b[:, 0:wide], sa, MULT)
+            if q > 0:
+                turn(flat(raw_chunk[1][q]), half, bank[3 + q][:, half:T])
 
         def last_chunk(b):
-            u = ring.tile([P, 2 * P], F32, name="u", tag="u", bufs=4)
+            u = ring.tile([P, 2 * P], F32, name="u", tag="u")
             weigh(CH - 1, b * P, P, u[:])
-            ct = bank[5 - b % 2][:, 0:P]
+            ct = bank[(7, whole % 2)[b % 2]][:, 0:P]
             turn(u[:], P, ct)
             nc.scalar.copy(cb[:, b, (CH - 1) * P :], ct)
 
         def finish(b):
             words = cb[:, b, :].bitcast(F32)
-            xt = bank[6 + b % 2][:, 0 : 2 * P].rearrange("p (u t) -> p u t", u=2)
+            xt = bank[4 + b % 2][:, 0 : 2 * P].rearrange("p (u t) -> p u t", u=2)
             for u in range(2):
                 nc.tensor.transpose(xt[:, u, :], words[:, u : H // 2 : 2], ident[:])
-            g = ring.tile([P, P, PACK], BF16, name="cg", tag="cg", align_bytes=64, bufs=4)
+            g = ring.tile([P, P, PACK], BF16, name="cg", tag="cg", align_bytes=64)
             nc.scalar.copy(
                 g[:].rearrange("p t j -> p (t j)").bitcast(F32).rearrange("p (t u) -> p t u", u=2),
                 xt.rearrange("p u t -> p t u"),
             )
             codes, scales = quantize(g, P)
-            for k in range(2):
-                o = bank[2 * (b % 2) + k]
-                for c in range(2):
-                    n0 = (2 * k + c) * P
-                    nc.tensor.matmul_mx(
-                        out=o[:, c * P : (c + 1) * P],
-                        lhsT=w2w[:, n0 : n0 + P].bitcast(FP8X4),
-                        lhsT_scale=w2s[:, n0 : n0 + P],
-                        rhs=codes[:].bitcast(FP8X4),
-                        rhs_scale=scales[:],
-                        start=True,
-                        stop=True,
-                    )
-                res = ring.tile([P, 2, P], F32, name="res", tag="res", bufs=8)
-                src = o[:, 0 : 2 * P].rearrange("p (c t) -> p c t", c=2)
-                if k == 0:
-                    nc.scalar.copy(res[:], src)
-                else:
-                    nc.vector.tensor_copy(res[:], src)
-                nc.sync.dma_start(
-                    out=out.rearrange("(c p) t -> p c t", p=P)[:, 2 * k : 2 * k + 2, b * P : (b + 1) * P],
-                    in_=res[:],
+            for c in range(N // P):
+                nc.tensor.matmul_mx(
+                    out=result_bank(b, c // 2)[:, c * P : (c + 1) * P],
+                    lhsT=w2w[:, c * P : (c + 1) * P].bitcast(FP8X4),
+                    lhsT_scale=w2s[:, c * P : (c + 1) * P],
+                    rhs=codes[:].bitcast(FP8X4),
+                    rhs_scale=scales[:],
+                    start=True,
+                    stop=True,
                 )
+
+        def result_bank(b, k):
+            if (b, k) == (TB - 1, 1):
+                return bank[7]
+            return bank[(2 + whole % 2, 6, 1 - whole % 2, 3 - whole % 2)[b]]
+
+        def store(b, k):
+            res = ring.tile([P, 2, P], F32, name="res", tag="res", bufs=8)
+            src = result_bank(b, k)[:, 2 * k * P : 2 * (k + 1) * P].rearrange("p (c t) -> p c t", c=2)
+            if b == TB - 2 or (b, k) == (TB - 1, 1):
+                nc.scalar.copy(res[:], src)
+            else:
+                nc.vector.tensor_copy(res[:], src)
+            nc.sync.dma_start(
+                out=out.rearrange("(c p) t -> p c t", p=P)[:, 2 * k : 2 * k + 2, b * P : (b + 1) * P],
+                in_=res[:],
+            )
 
         for e in range(whole):
             if e * C % XG == 0:
                 gather_tokens(e * C)
-            piece("s", 0, e, 0, H, bank[e % 2])
+            multiply(raw_whole[0][e], H, H, [e] * CH, bank[e % 2])
             if e > 0:
-                gate_whole(e - 1, flat(0, e, 0)[:, 0:H])
-            piece("v", 1, e, 0, H, bank[2 + e % 2])
+                gate_whole(e - 1, raw_whole[0][e])
+            multiply(raw_whole[1][e], H, W3_SCALAR_COLS, [e] * CH, bank[2 + e % 2])
+        gate_whole(whole - 1, raw_whole[1][whole - 1])
         for a in range(-(-whole * C // XG) * XG, S, XG):
             gather_tokens(a)
         for q in range(CH):
             split_chunk(q)
-        turn_chunk(CH - 2, bank[4])
+        for q in range(CH - 1):
+            nc.scalar.copy(cb[:, :, q * P : (q + 1) * P], bank[4 + q][:].rearrange("p (b c) -> p b c", c=P))
         for b in range(TB):
             last_chunk(b)
             if b > 0:
                 finish(b - 1)
         finish(TB - 1)
+        for b in range(TB):
+            for k in range(2):
+                store(b, k)

@@ -21,11 +21,8 @@ P = 128
 PACK = 4
 CH = H // P
 TB = T // P
-SPLIT = 3
+SPLIT = 2
 XG = 256
-W3_SCALAR_COLS = 128
-FIRST_VECTOR_COLS = 256
-LATER_VECTOR_COLS = 0
 
 
 def tile_moe_sdn_glu_silu_kernel(
@@ -33,11 +30,9 @@ def tile_moe_sdn_glu_silu_kernel(
 ):
     nc = tc.nc
     whole = E - SPLIT
-    wide = SPLIT * P
-    half = T // 2
     with ExitStack() as ctx:
         keep = ctx.enter_context(tc.tile_pool(name="keep", bufs=1))
-        ring = ctx.enter_context(tc.tile_pool(name="ring", bufs=4))
+        ring = ctx.enter_context(tc.tile_pool(name="ring", bufs=3))
         psum = ctx.enter_context(tc.psum_pool(name="psum", bufs=1))
         bank = [psum.tile([P, 512], F32, name=f"bank{i}") for i in range(8)]
 
@@ -49,13 +44,10 @@ def tile_moe_sdn_glu_silu_kernel(
         w2s = keep.tile([P, N], U8, name="w2s", align_bytes=64)
         xgw = keep.tile([P, S], U32, name="xgw", align_bytes=64)
         xgs = keep.tile([P, S], U8, name="xgs", align_bytes=64)
-        gate_sb = keep.tile([P, 2, T], F32, name="gate_sb")
         ident = keep.tile([P, P], F32, name="ident")
         warm = keep.tile([P, 8], F32, name="warm")
         h = [keep.tile([P, S], F32, name=f"h{q}") for q in range(CH)]
         cb = keep.tile([P, TB, H], BF16, name="cb", align_bytes=64)
-        raw_whole = [[keep.tile([P, PACK, H], F32, name=f"raw{m}_{e}") for e in range(whole)] for m in range(2)]
-        raw_chunk = [[keep.tile([P, PACK, wide], F32, name=f"rawc{m}_{q}") for q in range(CH)] for m in range(2)]
 
         nc.vector.memset(xs[:].bitcast(I32), 0)
         nc.vector.memset(warm[:], 0.0)
@@ -72,78 +64,91 @@ def tile_moe_sdn_glu_silu_kernel(
         def load_words(tile, words):
             nc.sync.dma_start(out=tile[:], in_=words.rearrange("p t d -> p (t d)").bitcast(I32))
 
-        def rows_of(m, e):
-            return (w1, w3)[m][e].rearrange("(p j) c -> p j c", j=PACK)
+        raw = {}
 
-        def load_chunk(m, q):
-            for u in range(SPLIT):
-                nc.sync.dma_start(
-                    out=raw_chunk[m][q][:, :, u * P : (u + 1) * P],
-                    in_=rows_of(m, whole + u)[:, :, q * P : (q + 1) * P],
-                )
+        def load_piece(m, e, c0, width):
+            src = (w1, w3)[m]
+            t = keep.tile([P, PACK, width], F32, name=f"raw{m}_{e}_{c0}")
+            nc.sync.dma_start(
+                out=t[:], in_=src[e].rearrange("(p j) c -> p j c", j=PACK)[:, :, c0 : c0 + width]
+            )
+            raw[(m, e, c0)] = t
 
         nc.sync.dma_start(offs_sb[:], offs)
         load_words(xw, x_words[0])
-        load_scales(nc.scalar, xs, x_scales[0])
+        load_scales(nc.sync, xs, x_scales[0])
         nc.scalar.activation(warm[:], warm[:], SILU)
-        for e in range(whole):
-            for m in range(2):
-                nc.sync.dma_start(out=raw_whole[m][e][:], in_=rows_of(m, e))
-        nc.sync.dma_start(pos_sb[0][:], pos1)
-        nc.sync.dma_start(pos_sb[1][:], pos2)
-        gate_rows = gate.rearrange("r p t -> p r t")
+        load_piece(0, 0, 0, H)
+        load_piece(1, 0, 0, H)
+        gate_col = keep.tile([P, 2, PACK], F32, name="gate_col")
+        nc.sync.dma_start(gate_col[:], gate[:, 0, :].rearrange("r (p j) -> p r j", j=PACK))
+        for e in range(1, whole):
+            load_piece(0, e, 0, H)
+            load_piece(1, e, 0, H)
         for q in range(CH):
             for m in range(2):
-                load_chunk(m, q)
-                if q == 1:
-                    cols = slice(m * half, (m + 1) * half)
-                    nc.sync.dma_start(gate_sb[:, :, cols], gate_rows[:, :, cols])
+                for e in range(whole, E):
+                    load_piece(m, e, q * P, P)
+            if q == 0:
+                nc.sync.dma_start(pos_sb[0][:], pos1)
+                nc.sync.dma_start(pos_sb[1][:], pos2)
         load_words(w2w, w2_words[0])
         load_scales(nc.sync, w2s, w2_scales[0])
+
+        gate_sb = raw[(0, 2, 0)][:, 2:4, :]
+
+        def spread_gate():
+            for r in range(2):
+                spread = bank[6 + r]
+                for j in range(PACK):
+                    nc.tensor.transpose(
+                        spread[:, j * P : (j + 1) * P], gate_col[:, r, j : j + 1].to_broadcast([P, P]), ident[:]
+                    )
+                nc.scalar.copy(
+                    gate_sb[:, r, :].rearrange("p (n j) -> p n j", j=PACK),
+                    spread[:].rearrange("p (j n) -> p n j", j=PACK),
+                )
 
         def gather_tokens(a):
             sl = offs_sb[:, a // 16 : (a + XG) // 16]
             nc.vector.tensor_copy(xgw[:, a : a + XG], xw[:].bitcast(U32).indirect(sl))
             nc.vector.tensor_copy(xgs[:, a : a + XG], xs[:].indirect(sl))
 
-        def flat(tile):
-            return tile[:].rearrange("p j c -> p (j c)")
+        def flat(m, e, c0):
+            return raw[(m, e, c0)][:].rearrange("p j c -> p (j c)")
 
         def quantize(g, width):
-            codes = ring.tile([P, width], U32, name="codes", tag=f"codes{width}", align_bytes=64)
-            scales = ring.tile([P, width], U8, name="scales", tag=f"scales{width}", align_bytes=64)
-            for a, b in ([(0, 256), (256, 384)] if width == 384 else [(0, width)]):
-                nc.vector.quantize_mx(
-                    out=codes[:, a:b].bitcast(FP8X4),
-                    scales=scales[:, a:b],
-                    in_=g[:, a:b, :].rearrange("p c j -> p (c j)"),
-                )
+            codes = ring.tile([P, width], U32, name="codes", tag=f"codes{width}", align_bytes=64, bufs=4)
+            scales = ring.tile([P, width], U8, name="scales", tag=f"scales{width}", align_bytes=64, bufs=4)
+            nc.vector.quantize_mx(
+                out=codes[:].bitcast(FP8X4), scales=scales[:], in_=g[:].rearrange("p c j -> p (c j)")
+            )
             return codes, scales
 
-        def multiply(raw, width, scalar_cols, experts, acc, g=None):
-            if g is None:
-                g = ring.tile([P, width, PACK], BF16, name="grouped", tag=f"grouped{width}", align_bytes=64)
+        def piece(scalar_cols, m, e, c0, width, acc):
+            if (m, e, c0) == (1, E - 1, H - P):
+                g = cb[:, 0, :].rearrange("p (c j) -> p c j", j=PACK)
+            else:
+                g = ring.tile([P, width, PACK], BF16, name="grouped", tag=f"grouped{width}", align_bytes=64, bufs=4)
             for a, b, copy in ((0, scalar_cols, nc.scalar.copy), (scalar_cols, width, nc.vector.tensor_copy)):
                 if b > a:
                     copy(
                         g[:, a:b, :].rearrange("p (c i) j -> p c j i", i=4),
-                        raw[:, :, a:b].rearrange("p j (c i) -> p c j i", i=4),
+                        raw[(m, e, c0)][:, :, a:b].rearrange("p j (c i) -> p c j i", i=4),
                     )
             codes, scales = quantize(g, width)
-            for k, e in enumerate(experts):
-                cols = slice(k * P, (k + 1) * P)
+            for a in range(0, width, P):
                 nc.tensor.matmul_mx(
-                    out=acc[:, cols],
-                    lhsT=codes[:, cols].bitcast(FP8X4),
-                    lhsT_scale=scales[:, cols],
+                    out=acc[:, a : a + C],
+                    lhsT=codes[:, a : a + P].bitcast(FP8X4),
+                    lhsT_scale=scales[:, a : a + P],
                     rhs=xgw[:, e * C : (e + 1) * C].bitcast(FP8X4),
                     rhs_scale=xgs[:, e * C : (e + 1) * C],
                     start=True,
                     stop=True,
                 )
 
-        def gate_whole(e, landing):
-            sa = landing[:, :, 0:C]
+        def gate_whole(e, sa):
             nc.scalar.activation(sa, bank[e % 2][:].rearrange("p (q c) -> p q c", c=C), SILU)
             for q in range(CH):
                 cols = slice(q * C, (q + 1) * C)
@@ -168,31 +173,30 @@ def tile_moe_sdn_glu_silu_kernel(
                         stop=(r == 1),
                     )
 
+        half = T // 2
 
         def split_chunk(q):
             k = whole + q
             a, b = bank[k % 2], bank[2 + k % 2]
-            experts = range(whole, E)
-            multiply(raw_chunk[0][q], wide, wide, experts, a)
+            for u in range(SPLIT):
+                piece(P, 0, whole + u, q * P, P, a[:, u * C : (u + 1) * C])
             if q > 0:
-                weigh(q - 1, 0, half, flat(raw_chunk[0][q]))
-                turn(flat(raw_chunk[0][q]), half, bank[3 + q][:, 0:half])
-            g = None
-            if q == CH - 1:
-                g = cb[:].rearrange("p b i -> p (b i)")[:, 0 : wide * PACK].rearrange("p (c j) -> p c j", j=PACK)
-            multiply(raw_chunk[1][q], wide, wide - (LATER_VECTOR_COLS if q else FIRST_VECTOR_COLS), experts, b, g)
-            sa = flat(raw_chunk[1][q])[:, T : T + wide]
-            nc.scalar.activation(sa, a[:, 0:wide], SILU)
+                weigh(q - 1, 0, half, flat(0, E - 1, q * P))
+                turn(flat(0, E - 1, q * P), half, bank[3 + q][:, 0:half])
+            for u in range(SPLIT):
+                piece(0 if q == 0 else P, 1, whole + u, q * P, P, b[:, u * C : (u + 1) * C])
+            sa = flat(1, whole, q * P)[:, 0 : SPLIT * C]
+            nc.scalar.activation(sa, a[:, 0 : SPLIT * C], SILU)
             if q > 0:
-                weigh(q - 1, half, half, flat(raw_chunk[1][q]))
-            nc.vector.tensor_tensor(h[q][:, whole * C :], b[:, 0:wide], sa, MULT)
+                weigh(q - 1, half, half, flat(1, E - 1, q * P))
+            nc.vector.tensor_tensor(h[q][:, whole * C :], b[:, 0 : SPLIT * C], sa, MULT)
             if q > 0:
-                turn(flat(raw_chunk[1][q]), half, bank[3 + q][:, half:T])
+                turn(flat(1, E - 1, q * P), half, bank[3 + q][:, half:T])
 
         def last_chunk(b):
-            u = ring.tile([P, 2 * P], F32, name="u", tag="u")
+            u = ring.tile([P, 2 * P], F32, name="u", tag="u", bufs=4)
             weigh(CH - 1, b * P, P, u[:])
-            ct = bank[(7, whole % 2)[b % 2]][:, 0:P]
+            ct = bank[(7, 0)[b % 2]][:, 0:P]
             turn(u[:], P, ct)
             nc.scalar.copy(cb[:, b, (CH - 1) * P :], ct)
 
@@ -201,7 +205,7 @@ def tile_moe_sdn_glu_silu_kernel(
             xt = bank[4 + b % 2][:, 0 : 2 * P].rearrange("p (u t) -> p u t", u=2)
             for u in range(2):
                 nc.tensor.transpose(xt[:, u, :], words[:, u : H // 2 : 2], ident[:])
-            g = ring.tile([P, P, PACK], BF16, name="cg", tag="cg", align_bytes=64)
+            g = ring.tile([P, P, PACK], BF16, name="cg", tag="cg", align_bytes=64, bufs=4)
             nc.scalar.copy(
                 g[:].rearrange("p t j -> p (t j)").bitcast(F32).rearrange("p (t u) -> p t u", u=2),
                 xt.rearrange("p u t -> p t u"),
@@ -221,7 +225,7 @@ def tile_moe_sdn_glu_silu_kernel(
         def result_bank(b, k):
             if (b, k) == (TB - 1, 1):
                 return bank[7]
-            return bank[(2 + whole % 2, 6, 1 - whole % 2, 3 - whole % 2)[b]]
+            return bank[(2, 6, 1, 3)[b]]
 
         def store(b, k):
             res = ring.tile([P, 2, P], F32, name="res", tag="res", bufs=8)
@@ -238,11 +242,13 @@ def tile_moe_sdn_glu_silu_kernel(
         for e in range(whole):
             if e * C % XG == 0:
                 gather_tokens(e * C)
-            multiply(raw_whole[0][e], H, H, [e] * CH, bank[e % 2])
+            piece(H, 0, e, 0, H, bank[e % 2])
             if e > 0:
-                gate_whole(e - 1, raw_whole[0][e])
-            multiply(raw_whole[1][e], H, W3_SCALAR_COLS, [e] * CH, bank[2 + e % 2])
-        gate_whole(whole - 1, raw_whole[1][whole - 1])
+                gate_whole(e - 1, raw[(0, e, 0)][:, 0, :].rearrange("p (q c) -> p q c", c=C))
+            piece(0, 1, e, 0, H, bank[2 + e % 2])
+            if e == 2:
+                spread_gate()
+        gate_whole(whole - 1, raw[(1, whole - 1, 0)][:, :, 0:C])
         for a in range(-(-whole * C // XG) * XG, S, XG):
             gather_tokens(a)
         for q in range(CH):

@@ -45,12 +45,10 @@ def tile_moe_sdn_glu_silu_kernel(
         xgw = keep.tile([P, S], U32, name="xgw", align_bytes=64)
         xgs = keep.tile([P, S], U8, name="xgs", align_bytes=64)
         ident = keep.tile([P, P], F32, name="ident")
-        warm = keep.tile([P, 8], F32, name="warm")
         h = [keep.tile([P, S], F32, name=f"h{q}") for q in range(CH)]
         cb = keep.tile([P, TB, H], BF16, name="cb", align_bytes=64)
 
         nc.vector.memset(xs[:].bitcast(I32), 0)
-        nc.vector.memset(warm[:], 0.0)
         nc.vector.memset(w2s[:].bitcast(I32), 0)
         make_identity(nc, ident[:])
 
@@ -77,7 +75,6 @@ def tile_moe_sdn_glu_silu_kernel(
         nc.sync.dma_start(offs_sb[:], offs)
         load_words(xw, x_words[0])
         load_scales(nc.sync, xs, x_scales[0])
-        nc.scalar.activation(warm[:], warm[:], SILU)
         load_piece(0, 0, 0, H)
         load_piece(1, 0, 0, H)
         gate_col = keep.tile([P, 2, PACK], F32, name="gate_col")
@@ -121,32 +118,49 @@ def tile_moe_sdn_glu_silu_kernel(
             codes = ring.tile([P, width], U32, name="codes", tag=f"codes{width}", align_bytes=64, bufs=4)
             scales = ring.tile([P, width], U8, name="scales", tag=f"scales{width}", align_bytes=64, bufs=4)
             nc.vector.quantize_mx(
-                out=codes[:].bitcast(FP8X4), scales=scales[:], in_=g[:].rearrange("p c j -> p (c j)")
+                out=codes[:].bitcast(FP8X4), scales=scales[:], in_=g.rearrange("p c j -> p (c j)")
             )
             return codes, scales
 
-        def piece(scalar_cols, m, e, c0, width, acc):
-            if (m, e, c0) == (1, E - 1, H - P):
-                g = cb[:, 0, :].rearrange("p (c j) -> p c j", j=PACK)
-            else:
-                g = ring.tile([P, width, PACK], BF16, name="grouped", tag=f"grouped{width}", align_bytes=64, bufs=4)
+        def cast(g, m, e, c0, scalar_cols):
+            width = g.shape[1]
             for a, b, copy in ((0, scalar_cols, nc.scalar.copy), (scalar_cols, width, nc.vector.tensor_copy)):
                 if b > a:
                     copy(
                         g[:, a:b, :].rearrange("p (c i) j -> p c j i", i=4),
                         raw[(m, e, c0)][:, :, a:b].rearrange("p j (c i) -> p c j i", i=4),
                     )
-            codes, scales = quantize(g, width)
-            for a in range(0, width, P):
+
+        def multiply(g, experts, acc):
+            codes, scales = quantize(g, len(experts) * P)
+            for a, e in enumerate(experts):
                 nc.tensor.matmul_mx(
-                    out=acc[:, a : a + C],
-                    lhsT=codes[:, a : a + P].bitcast(FP8X4),
-                    lhsT_scale=scales[:, a : a + P],
+                    out=acc[:, a * C : (a + 1) * C],
+                    lhsT=codes[:, a * P : (a + 1) * P].bitcast(FP8X4),
+                    lhsT_scale=scales[:, a * P : (a + 1) * P],
                     rhs=xgw[:, e * C : (e + 1) * C].bitcast(FP8X4),
                     rhs_scale=xgs[:, e * C : (e + 1) * C],
                     start=True,
                     stop=True,
                 )
+
+        def grouped(width):
+            g = ring.tile([P, width, PACK], BF16, name="grouped", tag=f"grouped{width}", align_bytes=64, bufs=4)
+            return g[:]
+
+        def piece(scalar_cols, m, e, c0, width, acc):
+            if (m, e, c0) == (1, E - 1, H - P):
+                g = cb[:, 0, :].rearrange("p (c j) -> p c j", j=PACK)
+            else:
+                g = grouped(width)
+            cast(g, m, e, c0, scalar_cols)
+            multiply(g, [e] * (width // P), acc)
+
+        def pair(scalar_cols, m, q, acc):
+            g = grouped(SPLIT * P)
+            for u in range(SPLIT):
+                cast(g[:, u * P : (u + 1) * P, :], m, whole + u, q * P, scalar_cols[u])
+            multiply(g, list(range(whole, E)), acc)
 
         def gate_whole(e, sa):
             nc.scalar.activation(sa, bank[e % 2][:].rearrange("p (q c) -> p q c", c=C), SILU)
@@ -175,22 +189,35 @@ def tile_moe_sdn_glu_silu_kernel(
 
         half = T // 2
 
+        def gate_split(q, sa):
+            k = whole + q
+            nc.scalar.activation(sa, bank[k % 2][:, 0 : SPLIT * C], SILU)
+            if q > 0:
+                weigh(q - 1, half, half, flat(1, E - 1, q * P))
+            nc.vector.tensor_tensor(h[q][:, whole * C :], bank[2 + k % 2][:, 0 : SPLIT * C], sa, MULT)
+
         def split_chunk(q):
             k = whole + q
             a, b = bank[k % 2], bank[2 + k % 2]
-            for u in range(SPLIT):
-                piece(P, 0, whole + u, q * P, P, a[:, u * C : (u + 1) * C])
-            if q > 0:
+            if q == 1:
+                for u in range(SPLIT):
+                    piece(P, 0, whole + u, q * P, P, a[:, u * C : (u + 1) * C])
+                    if u == 0:
+                        gate_split(0, flat(0, whole, P)[:, 0 : SPLIT * C])
+            else:
+                pair((P, P), 0, q, a)
+            if q == 0:
+                gate_whole(whole - 1, raw[(0, E - 1, 0)][:])
+            else:
                 weigh(q - 1, 0, half, flat(0, E - 1, q * P))
                 turn(flat(0, E - 1, q * P), half, bank[3 + q][:, 0:half])
-            for u in range(SPLIT):
-                piece(0 if q == 0 else P, 1, whole + u, q * P, P, b[:, u * C : (u + 1) * C])
-            sa = flat(1, whole, q * P)[:, 0 : SPLIT * C]
-            nc.scalar.activation(sa, a[:, 0 : SPLIT * C], SILU)
+            if q < CH - 1:
+                pair((P, 0 if q == 0 else P), 1, q, b)
+            else:
+                for u in range(SPLIT):
+                    piece(P, 1, whole + u, q * P, P, b[:, u * C : (u + 1) * C])
             if q > 0:
-                weigh(q - 1, half, half, flat(1, E - 1, q * P))
-            nc.vector.tensor_tensor(h[q][:, whole * C :], b[:, 0 : SPLIT * C], sa, MULT)
-            if q > 0:
+                gate_split(q, flat(1, whole, q * P)[:, 0 : SPLIT * C])
                 turn(flat(1, E - 1, q * P), half, bank[3 + q][:, half:T])
 
         def last_chunk(b):
@@ -210,7 +237,7 @@ def tile_moe_sdn_glu_silu_kernel(
                 g[:].rearrange("p t j -> p (t j)").bitcast(F32).rearrange("p (t u) -> p t u", u=2),
                 xt.rearrange("p u t -> p t u"),
             )
-            codes, scales = quantize(g, P)
+            codes, scales = quantize(g[:], P)
             for c in range(N // P):
                 nc.tensor.matmul_mx(
                     out=result_bank(b, c // 2)[:, c * P : (c + 1) * P],
@@ -239,18 +266,15 @@ def tile_moe_sdn_glu_silu_kernel(
                 in_=res[:],
             )
 
+        for a in range(0, S, XG):
+            gather_tokens(a)
         for e in range(whole):
-            if e * C % XG == 0:
-                gather_tokens(e * C)
-            piece(H, 0, e, 0, H, bank[e % 2])
+            piece(320, 0, e, 0, H, bank[e % 2])
             if e > 0:
                 gate_whole(e - 1, raw[(0, e, 0)][:, 0, :].rearrange("p (q c) -> p q c", c=C))
-            piece(0, 1, e, 0, H, bank[2 + e % 2])
+            piece(320 if e < whole - 1 else 192, 1, e, 0, H, bank[2 + e % 2])
             if e == 2:
                 spread_gate()
-        gate_whole(whole - 1, raw[(1, whole - 1, 0)][:, :, 0:C])
-        for a in range(-(-whole * C // XG) * XG, S, XG):
-            gather_tokens(a)
         for q in range(CH):
             split_chunk(q)
         for q in range(CH - 1):

@@ -74,8 +74,8 @@ def tile_moe_sdn_glu_silu_kernel(
 
         nc.sync.dma_start(offs_sb[:], offs)
         load_words(xw, x_words[0])
-        load_scales(nc.sync, xs, x_scales[0])
         load_piece(0, 0, 0, H)
+        load_scales(nc.sync, xs, x_scales[0])
         load_piece(1, 0, 0, H)
         gate_col = keep.tile([P, 2, PACK], F32, name="gate_col")
         nc.sync.dma_start(gate_col[:], gate[:, 0, :].rearrange("r (p j) -> p r j", j=PACK))
@@ -220,49 +220,55 @@ def tile_moe_sdn_glu_silu_kernel(
                 gate_split(q, flat(1, whole, q * P)[:, 0 : SPLIT * C])
                 turn(flat(1, E - 1, q * P), half, bank[3 + q][:, half:T])
 
+        def rounded(b0, nb, q):
+            return cb[:, b0 : b0 + nb, :].rearrange("p b (u m e) -> p b u m e", u=2, e=2)[:, :, :, 32 * q : 32 * (q + 1), :]
+
+        def round_sum(b0, nb, q, src):
+            nc.scalar.copy(rounded(b0, nb, q), src.rearrange("p (b m u e) -> p b u m e", b=nb, u=2, e=2))
+
         def last_chunk(b):
             u = ring.tile([P, 2 * P], F32, name="u", tag="u", bufs=4)
             weigh(CH - 1, b * P, P, u[:])
             ct = bank[(7, 0)[b % 2]][:, 0:P]
             turn(u[:], P, ct)
-            nc.scalar.copy(cb[:, b, (CH - 1) * P :], ct)
+            round_sum(b, 1, CH - 1, ct)
 
-        def finish(b):
+        c_codes = [keep.tile([P, 2 * P], U32, name=f"c_codes{i}", align_bytes=64) for i in range(2)]
+        c_scales = [keep.tile([P, 2 * P], U8, name=f"c_scales{i}", align_bytes=64) for i in range(2)]
+
+        def turn_back(b):
             words = cb[:, b, :].bitcast(F32)
-            xt = bank[4 + b % 2][:, 0 : 2 * P].rearrange("p (u t) -> p u t", u=2)
+            xt = bank[(2, 4, 5, 1)[b]][:, 0 : 2 * P].rearrange("p (u t) -> p u t", u=2)
             for u in range(2):
-                nc.tensor.transpose(xt[:, u, :], words[:, u : H // 2 : 2], ident[:])
+                nc.tensor.transpose(xt[:, u, :], words[:, u * P : (u + 1) * P], ident[:])
             g = ring.tile([P, P, PACK], BF16, name="cg", tag="cg", align_bytes=64, bufs=4)
             nc.scalar.copy(
                 g[:].rearrange("p t j -> p (t j)").bitcast(F32).rearrange("p (t u) -> p t u", u=2),
                 xt.rearrange("p u t -> p t u"),
             )
-            codes, scales = quantize(g[:], P)
-            for c in range(N // P):
-                nc.tensor.matmul_mx(
-                    out=result_bank(b, c // 2)[:, c * P : (c + 1) * P],
-                    lhsT=w2w[:, c * P : (c + 1) * P].bitcast(FP8X4),
-                    lhsT_scale=w2s[:, c * P : (c + 1) * P],
-                    rhs=codes[:].bitcast(FP8X4),
-                    rhs_scale=scales[:],
-                    start=True,
-                    stop=True,
-                )
+            cols = slice((b % 2) * P, (b % 2 + 1) * P)
+            nc.vector.quantize_mx(
+                out=c_codes[b // 2][:, cols].bitcast(FP8X4),
+                scales=c_scales[b // 2][:, cols],
+                in_=g[:].rearrange("p c j -> p (c j)"),
+            )
 
-        def result_bank(b, k):
-            if (b, k) == (TB - 1, 1):
-                return bank[7]
-            return bank[(2, 6, 1, 3)[b]]
+        def project(i, c, acc):
+            nc.tensor.matmul_mx(
+                out=acc,
+                lhsT=w2w[:, c * P : (c + 1) * P].bitcast(FP8X4),
+                lhsT_scale=w2s[:, c * P : (c + 1) * P],
+                rhs=c_codes[i][:].bitcast(FP8X4),
+                rhs_scale=c_scales[i][:],
+                start=True,
+                stop=True,
+            )
 
-        def store(b, k):
-            res = ring.tile([P, 2, P], F32, name="res", tag="res", bufs=8)
-            src = result_bank(b, k)[:, 2 * k * P : 2 * (k + 1) * P].rearrange("p (c t) -> p c t", c=2)
-            if b == TB - 2 or (b, k) == (TB - 1, 1):
-                nc.scalar.copy(res[:], src)
-            else:
-                nc.vector.tensor_copy(res[:], src)
+        def store(i, c0, n, src, copy):
+            res = keep.tile([P, n, half], F32, name=f"res{i}_{c0}")
+            copy(res[:], src.rearrange("p (c t) -> p c t", c=n))
             nc.sync.dma_start(
-                out=out.rearrange("(c p) t -> p c t", p=P)[:, 2 * k : 2 * k + 2, b * P : (b + 1) * P],
+                out=out.rearrange("(c p) t -> p c t", p=P)[:, c0 : c0 + n, i * half : (i + 1) * half],
                 in_=res[:],
             )
 
@@ -278,12 +284,20 @@ def tile_moe_sdn_glu_silu_kernel(
         for q in range(CH):
             split_chunk(q)
         for q in range(CH - 1):
-            nc.scalar.copy(cb[:, :, q * P : (q + 1) * P], bank[4 + q][:].rearrange("p (b c) -> p b c", c=P))
-        for b in range(TB):
-            last_chunk(b)
-            if b > 0:
-                finish(b - 1)
-        finish(TB - 1)
-        for b in range(TB):
-            for k in range(2):
-                store(b, k)
+            round_sum(0, TB, q, bank[4 + q][:])
+        last_chunk(0)
+        last_chunk(1)
+        turn_back(0)
+        last_chunk(2)
+        turn_back(1)
+        last_chunk(3)
+        turn_back(2)
+        turn_back(3)
+        for c in range(4):
+            project(0, c, bank[(0, 7)[c // 2]][:, (c % 2) * half : (c % 2 + 1) * half])
+        for c in range(4):
+            project(1, c, bank[(3, 6, 2, 4)[c]][:, 0:half])
+        store(0, 0, 2, bank[0][:], nc.scalar.copy)
+        store(0, 2, 2, bank[7][:], nc.vector.tensor_copy)
+        for c in range(4):
+            store(1, c, 1, bank[(3, 6, 2, 4)[c]][:, 0:half], (nc.scalar.copy, nc.vector.tensor_copy)[c % 2])

@@ -127,8 +127,8 @@ def tile_moe_sdn_glu_silu_kernel(
             for a, b, copy in ((0, scalar_cols, nc.scalar.copy), (scalar_cols, width, nc.vector.tensor_copy)):
                 if b > a:
                     copy(
-                        g[:, a:b, :].rearrange("p (c i) j -> p c j i", i=4),
-                        raw[(m, e, c0)][:, :, a:b].rearrange("p j (c i) -> p c j i", i=4),
+                        g[:, a:b, :].rearrange("p (c i) j -> p c j i", i=2),
+                        raw[(m, e, c0)][:, :, a:b].rearrange("p j (c i) -> p c j i", i=2),
                     )
 
         def multiply(g, experts, acc):

@@ -15,21 +15,21 @@ U16 = mybir.dt.uint16
 U8 = mybir.dt.uint8
 FP8X4 = mybir.dt.float8_e4m3fn_x4
 SILU = mybir.ActivationFunctionType.Silu
+COPY = mybir.ActivationFunctionType.Copy
 MULT = mybir.AluOpType.mult
+ADD = mybir.AluOpType.add
 
 P = 128
 PACK = 4
-CH = H // P
-TB = T // P
-SPLIT = 2
 XG = 256
+SCALAR_COLS = 288
+SCALAR_COLS_LAST = 176
 
 
 def tile_moe_sdn_glu_silu_kernel(
     tc, x_words, x_scales, w1, w3, w2_words, w2_scales, gate, offs, pos1, pos2, out
 ):
     nc = tc.nc
-    whole = E - SPLIT
     with ExitStack() as ctx:
         keep = ctx.enter_context(tc.tile_pool(name="keep", bufs=1))
         ring = ctx.enter_context(tc.tile_pool(name="ring", bufs=3))
@@ -42,19 +42,21 @@ def tile_moe_sdn_glu_silu_kernel(
         xs = keep.tile([P, T], U8, name="xs", align_bytes=64)
         w2w = keep.tile([P, N], I32, name="w2w", align_bytes=64)
         w2s = keep.tile([P, N], U8, name="w2s", align_bytes=64)
-        xgw = keep.tile([P, S], U32, name="xgw", align_bytes=64)
-        xgs = keep.tile([P, S], U8, name="xgs", align_bytes=64)
+        xgw, xgs = {}, {}
         ident = keep.tile([P, P], F32, name="ident")
-        h = [keep.tile([P, S], F32, name=f"h{q}") for q in range(CH)]
-        cb = keep.tile([P, TB, H], BF16, name="cb", align_bytes=64)
+        h = [keep.tile([P, S], F32, name=f"h{t}") for t in range(PACK)]
+        gate_rows = keep.tile([P, 2, 2 * P], F32, name="gate_rows")
+        gate_line = keep.tile([P, 2, 2 * P], F32, name="gate_line")
+        gate_cols = keep.tile([P, 4], F32, name="gate_cols")
 
         nc.vector.memset(xs[:].bitcast(I32), 0)
         nc.vector.memset(w2s[:].bitcast(I32), 0)
+        nc.vector.memset(gate_line[:], 0.0)
         make_identity(nc, ident[:])
 
-        def load_scales(engine, plane, rows):
+        def load_scales(plane, rows):
             for g in range(4):
-                engine.dma_start(
+                nc.sync.dma_start(
                     out=plane[32 * g : 32 * g + 4, :].bitcast(I32),
                     in_=rows[4 * g : 4 * g + 4, :].bitcast(I32),
                 )
@@ -64,240 +66,230 @@ def tile_moe_sdn_glu_silu_kernel(
 
         raw = {}
 
-        def load_piece(m, e, c0, width):
-            src = (w1, w3)[m]
-            t = keep.tile([P, PACK, width], F32, name=f"raw{m}_{e}_{c0}")
-            nc.sync.dma_start(
-                out=t[:], in_=src[e].rearrange("(p j) c -> p j c", j=PACK)[:, :, c0 : c0 + width]
-            )
-            raw[(m, e, c0)] = t
+        def load_matrix(m, e):
+            t = keep.tile([P, PACK, H], F32, name=f"raw{m}_{e}")
+            nc.sync.dma_start(out=t[:], in_=(w1, w3)[m][e].rearrange("(p j) c -> p j c", j=PACK))
+            raw[(m, e)] = t
 
         nc.sync.dma_start(offs_sb[:], offs)
         load_words(xw, x_words[0])
-        load_piece(0, 0, 0, H)
-        load_scales(nc.sync, xs, x_scales[0])
-        load_piece(1, 0, 0, H)
-        gate_col = keep.tile([P, 2, PACK], F32, name="gate_col")
-        nc.sync.dma_start(gate_col[:], gate[:, 0, :].rearrange("r (p j) -> p r j", j=PACK))
-        for e in range(1, whole):
-            load_piece(0, e, 0, H)
-            load_piece(1, e, 0, H)
-        for q in range(CH):
-            for m in range(2):
-                for e in range(whole, E):
-                    load_piece(m, e, q * P, P)
-            if q == 0:
-                nc.sync.dma_start(pos_sb[0][:], pos1)
-                nc.sync.dma_start(pos_sb[1][:], pos2)
+        load_matrix(0, 0)
+        load_scales(xs, x_scales[0])
+        load_matrix(1, 0)
+        nc.sync.dma_start(gate_line[0:1], gate[:, 0:1, 0 : 2 * P].rearrange("r p t -> p r t"))
+        for e in range(1, E):
+            load_matrix(0, e)
+            load_matrix(1, e)
+        nc.sync.dma_start(pos_sb[0][:], pos1)
+        nc.sync.dma_start(pos_sb[1][:], pos2)
+        nc.sync.dma_start(gate_rows[:], gate[:, :, 2 * P :].rearrange("r p t -> p r t"))
         load_words(w2w, w2_words[0])
-        load_scales(nc.sync, w2s, w2_scales[0])
+        load_scales(w2s, w2_scales[0])
 
-        gate_sb = raw[(0, 2, 0)][:, 2:4, :]
+        def gather_words(i):
+            xgw[i] = keep.tile([P, XG], U32, name="xgw", tag=f"words{i}", align_bytes=64)
+            nc.vector.tensor_copy(xgw[i][:], xw[:].bitcast(U32).indirect(offs_sb[:, i * XG // 16 : (i + 1) * XG // 16]))
 
-        def spread_gate():
-            for r in range(2):
-                spread = bank[6 + r]
-                for j in range(PACK):
-                    nc.tensor.transpose(
-                        spread[:, j * P : (j + 1) * P], gate_col[:, r, j : j + 1].to_broadcast([P, P]), ident[:]
-                    )
-                nc.scalar.copy(
-                    gate_sb[:, r, :].rearrange("p (n j) -> p n j", j=PACK),
-                    spread[:].rearrange("p (j n) -> p n j", j=PACK),
-                )
+        def gather_bytes(i):
+            xgs[i] = keep.tile([P, XG], U8, name="xgs", tag=f"bytes{i}", align_bytes=64)
+            nc.vector.tensor_copy(xgs[i][:], xs[:].indirect(offs_sb[:, i * XG // 16 : (i + 1) * XG // 16]))
 
-        def gather_tokens(a):
-            sl = offs_sb[:, a // 16 : (a + XG) // 16]
-            nc.vector.tensor_copy(xgw[:, a : a + XG], xw[:].bitcast(U32).indirect(sl))
-            nc.vector.tensor_copy(xgs[:, a : a + XG], xs[:].indirect(sl))
-
-        def flat(m, e, c0):
-            return raw[(m, e, c0)][:].rearrange("p j c -> p (j c)")
-
-        def quantize(g, width):
-            codes = ring.tile([P, width], U32, name="codes", tag=f"codes{width}", align_bytes=64, bufs=4)
-            scales = ring.tile([P, width], U8, name="scales", tag=f"scales{width}", align_bytes=64, bufs=4)
-            nc.vector.quantize_mx(
-                out=codes[:].bitcast(FP8X4), scales=scales[:], in_=g.rearrange("p c j -> p (c j)")
-            )
+        def quantize(src, width, tag):
+            codes = ring.tile([P, width], U32, name="codes", tag=f"codes{tag}", align_bytes=64, bufs=4)
+            scales = ring.tile([P, width], U8, name="scales", tag=f"scales{tag}", align_bytes=64, bufs=4)
+            nc.vector.quantize_mx(out=codes[:].bitcast(FP8X4), scales=scales[:], in_=src)
             return codes, scales
 
-        def cast(g, m, e, c0, scalar_cols):
-            width = g.shape[1]
-            for a, b, copy in ((0, scalar_cols, nc.scalar.copy), (scalar_cols, width, nc.vector.tensor_copy)):
-                if b > a:
-                    copy(
-                        g[:, a:b, :].rearrange("p (c i) j -> p c j i", i=2),
-                        raw[(m, e, c0)][:, :, a:b].rearrange("p j (c i) -> p c j i", i=2),
-                    )
+        def cast(m, e, scalar_cols, slot=None):
+            if slot is None:
+                g = ring.tile([P, PACK, P, PACK], BF16, name="grouped", tag="grouped", align_bytes=64, bufs=4)
+            else:
+                g = keep.tile([P, PACK, P, PACK], BF16, name="grouped", tag=slot, align_bytes=64)
+            src = raw[(m, e)][:].rearrange("p j (m t) -> p m j t", t=PACK)
+            dst = g[:].rearrange("p t m j -> p m j t")
+            cut = scalar_cols // PACK
+            nc.scalar.copy(dst[:, 0:cut], src[:, 0:cut])
+            nc.vector.tensor_copy(dst[:, cut:P], src[:, cut:P])
+            return g
 
-        def multiply(g, experts, acc):
-            codes, scales = quantize(g, len(experts) * P)
-            for a, e in enumerate(experts):
+        def multiply(g, e, t0, nt, acc):
+            codes, scales = quantize(g[:, t0 : t0 + nt].rearrange("p t m j -> p (t m j)"), nt * P, f"w{nt}")
+            cols = slice((e % 2) * C, (e % 2 + 1) * C)
+            for a in range(nt):
                 nc.tensor.matmul_mx(
                     out=acc[:, a * C : (a + 1) * C],
                     lhsT=codes[:, a * P : (a + 1) * P].bitcast(FP8X4),
                     lhsT_scale=scales[:, a * P : (a + 1) * P],
-                    rhs=xgw[:, e * C : (e + 1) * C].bitcast(FP8X4),
-                    rhs_scale=xgs[:, e * C : (e + 1) * C],
+                    rhs=xgw[e // 2][:, cols].bitcast(FP8X4),
+                    rhs_scale=xgs[e // 2][:, cols],
                     start=True,
                     stop=True,
                 )
 
-        def grouped(width):
-            g = ring.tile([P, width, PACK], BF16, name="grouped", tag=f"grouped{width}", align_bytes=64, bufs=4)
-            return g[:]
+        def silu(e, after):
+            sa = raw[after][:, :, 0:C]
+            nc.scalar.activation(sa, bank[e % 2][:].rearrange("p (t c) -> p t c", c=C), SILU)
+            return sa
 
-        def piece(scalar_cols, m, e, c0, width, acc):
-            if (m, e, c0) == (1, E - 1, H - P):
-                g = cb[:, 0, :].rearrange("p (c j) -> p c j", j=PACK)
+        def product(e, t, sa, acc):
+            nc.vector.tensor_tensor(h[t][:, e * C : (e + 1) * C], acc, sa[:, t, :], MULT)
+
+        def offsets(r, t0, n):
+            return pos_sb[r][:, t0 // 16 : (t0 + n) // 16]
+
+        plain = raw[(0, 0)][:].rearrange("p t (r c) -> p t r c", r=2)
+        direct = keep.tile([P, 22 * P], F32, name="direct", align_bytes=64)
+        weighed = [direct[:, a * P : (a + 8) * P].rearrange("p (t c) -> p t c", t=PACK) for a in (0, 11)]
+
+        def turned(b, r):
+            return bank[4 + 2 * b + r]
+
+        def plain_gather(b, nb, r, t, on_scalar=True, picked=None):
+            if picked is None:
+                picked = plain[:, t, r, b * P : (b + nb) * P]
+            window = h[t][:].indirect(offsets(r, b * P, nb * P))
+            if on_scalar:
+                nc.scalar.activation(picked, window, COPY)
             else:
-                g = grouped(width)
-            cast(g, m, e, c0, scalar_cols)
-            multiply(g, [e] * (width // P), acc)
+                nc.vector.tensor_copy(picked, window)
+            col = P * (t // 2) + 2 * P * (t % 2)
+            for a in range(nb):
+                nc.tensor.transpose(turned(b + a, r)[:, col : col + P], picked[:, a * P : (a + 1) * P], ident[:])
 
-        def pair(scalar_cols, m, q, acc):
-            g = grouped(SPLIT * P)
-            for u in range(SPLIT):
-                cast(g[:, u * P : (u + 1) * P, :], m, whole + u, q * P, scalar_cols[u])
-            multiply(g, list(range(whole, E)), acc)
+        def gated_gather(b, nb, r, t):
+            cols = slice((b - 2) * P, (b - 2 + nb) * P)
+            nc.vector.tensor_tensor(
+                weighed[r][:, t, cols], h[t][:].indirect(offsets(r, b * P, nb * P)), gate_rows[:, r, cols], MULT
+            )
 
-        def gate_whole(e, sa):
-            nc.scalar.activation(sa, bank[e % 2][:].rearrange("p (q c) -> p q c", c=C), SILU)
-            for q in range(CH):
-                cols = slice(q * C, (q + 1) * C)
-                nc.vector.tensor_tensor(h[q][:, e * C : (e + 1) * C], bank[2 + e % 2][:, cols], sa[:, q, :], MULT)
+        first = [direct[:, 7 * P : 11 * P], direct[:, 18 * P : 22 * P]]
+        summed = [keep.tile([P, H], BF16, name=f"summed{b}", align_bytes=64) for b in range(2)]
+        apart = [keep.tile([P, H], BF16, name=f"apart{b}", align_bytes=64) for b in range(3)]
+        cg = [apart[b % 3][:] for b in range(4)]
 
-        def weigh(q, t0, width, dst):
-            for r in range(2):
-                sl = pos_sb[r][:, t0 // 16 : (t0 + width) // 16]
-                nc.vector.tensor_tensor(
-                    dst[:, r * width : (r + 1) * width], h[q][:].indirect(sl), gate_sb[:, r, t0 : t0 + width], MULT
+        def scale_first(b):
+            nc.scalar.activation(
+                first[b].rearrange("p (w e) -> p w e", e=2),
+                turned(b, 0)[:].rearrange("p (e w) -> p w e", e=2),
+                COPY,
+                scale=gate_cols[:, b : b + 1],
+            )
+
+        def add_second(b):
+            nc.vector.scalar_tensor_tensor(
+                summed[b][:].rearrange("p (w e) -> p w e", e=2),
+                turned(b, 1)[:].rearrange("p (e w) -> p w e", e=2),
+                gate_cols[:, 2 + b : 3 + b],
+                first[b].rearrange("p (w e) -> p w e", e=2),
+                MULT,
+                ADD,
+            )
+            words = summed[b][:].bitcast(F32)
+            for u in range(2):
+                nc.tensor.transpose(bank[b][:, u * P : (u + 1) * P], words[:, u * P : (u + 1) * P], ident[:])
+
+        def copy_back(b):
+            nc.scalar.copy(
+                cg[b].bitcast(F32).rearrange("p (t u) -> p t u", u=2),
+                bank[b][:, 0 : 2 * P].rearrange("p (u t) -> p t u", u=2),
+            )
+
+        def add_both(b):
+            nc.vector.tensor_tensor(
+                cg[b].rearrange("p (c i t) -> p c t i", i=2, t=PACK),
+                weighed[0][:, :, (b - 2) * P : (b - 1) * P].rearrange("p t (c i) -> p c t i", i=2),
+                weighed[1][:, :, (b - 2) * P : (b - 1) * P].rearrange("p t (c i) -> p c t i", i=2),
+                ADD,
+            )
+
+        def project(b, accs):
+            codes, scales = quantize(cg[b], P, "c")
+            for c in range(4):
+                nc.tensor.matmul_mx(
+                    out=accs[c],
+                    lhsT=w2w[:, c * P : (c + 1) * P].bitcast(FP8X4),
+                    lhsT_scale=w2s[:, c * P : (c + 1) * P],
+                    rhs=codes[:].bitcast(FP8X4),
+                    rhs_scale=scales[:],
+                    start=True,
+                    stop=True,
                 )
 
-        def turn(src, width, ct):
-            for a in range(0, width, P):
-                for r in range(2):
-                    nc.tensor.matmul(
-                        ct[:, a : a + P],
-                        lhsT=src[:, r * width + a : r * width + a + P],
-                        rhs=ident[:],
-                        is_transpose=True,
-                        start=(r == 0),
-                        stop=(r == 1),
-                    )
+        def quarters(bk):
+            return [bk[:, c * P : (c + 1) * P] for c in range(4)]
 
-        half = T // 2
-
-        def gate_split(q, sa):
-            k = whole + q
-            nc.scalar.activation(sa, bank[k % 2][:, 0 : SPLIT * C], SILU)
-            if q > 0:
-                weigh(q - 1, half, half, flat(1, E - 1, q * P))
-            nc.vector.tensor_tensor(h[q][:, whole * C :], bank[2 + k % 2][:, 0 : SPLIT * C], sa, MULT)
-
-        def split_chunk(q):
-            k = whole + q
-            a, b = bank[k % 2], bank[2 + k % 2]
-            if q == 1:
-                for u in range(SPLIT):
-                    piece(P, 0, whole + u, q * P, P, a[:, u * C : (u + 1) * C])
-                    if u == 0:
-                        gate_split(0, flat(0, whole, P)[:, 0 : SPLIT * C])
-            else:
-                pair((P, P), 0, q, a)
-            if q == 0:
-                gate_whole(whole - 1, raw[(0, E - 1, 0)][:])
-            else:
-                weigh(q - 1, 0, half, flat(0, E - 1, q * P))
-                turn(flat(0, E - 1, q * P), half, bank[3 + q][:, 0:half])
-            if q < CH - 1:
-                pair((P, 0 if q == 0 else P), 1, q, b)
-            else:
-                for u in range(SPLIT):
-                    piece(P, 1, whole + u, q * P, P, b[:, u * C : (u + 1) * C])
-            if q > 0:
-                gate_split(q, flat(1, whole, q * P)[:, 0 : SPLIT * C])
-                turn(flat(1, E - 1, q * P), half, bank[3 + q][:, half:T])
-
-        def rounded(b0, nb, q):
-            return cb[:, b0 : b0 + nb, :].rearrange("p b (u m e) -> p b u m e", u=2, e=2)[:, :, :, 32 * q : 32 * (q + 1), :]
-
-        def round_sum(b0, nb, q, src):
-            nc.scalar.copy(rounded(b0, nb, q), src.rearrange("p (b m u e) -> p b u m e", b=nb, u=2, e=2))
-
-        def last_chunk(b):
-            u = ring.tile([P, 2 * P], F32, name="u", tag="u", bufs=4)
-            weigh(CH - 1, b * P, P, u[:])
-            ct = bank[(7, 0)[b % 2]][:, 0:P]
-            turn(u[:], P, ct)
-            round_sum(b, 1, CH - 1, ct)
-
-        c_codes = [keep.tile([P, 2 * P], U32, name=f"c_codes{i}", align_bytes=64) for i in range(2)]
-        c_scales = [keep.tile([P, 2 * P], U8, name=f"c_scales{i}", align_bytes=64) for i in range(2)]
-
-        def turn_back(b):
-            words = cb[:, b, :].bitcast(F32)
-            xt = bank[(2, 4, 5, 1)[b]][:, 0 : 2 * P].rearrange("p (u t) -> p u t", u=2)
-            for u in range(2):
-                nc.tensor.transpose(xt[:, u, :], words[:, u * P : (u + 1) * P], ident[:])
-            g = ring.tile([P, P, PACK], BF16, name="cg", tag="cg", align_bytes=64, bufs=4)
-            nc.scalar.copy(
-                g[:].rearrange("p t j -> p (t j)").bitcast(F32).rearrange("p (t u) -> p t u", u=2),
-                xt.rearrange("p u t -> p t u"),
-            )
-            cols = slice((b % 2) * P, (b % 2 + 1) * P)
-            nc.vector.quantize_mx(
-                out=c_codes[b // 2][:, cols].bitcast(FP8X4),
-                scales=c_scales[b // 2][:, cols],
-                in_=g[:].rearrange("p c j -> p (c j)"),
-            )
-
-        def project(i, c, acc):
-            nc.tensor.matmul_mx(
-                out=acc,
-                lhsT=w2w[:, c * P : (c + 1) * P].bitcast(FP8X4),
-                lhsT_scale=w2s[:, c * P : (c + 1) * P],
-                rhs=c_codes[i][:].bitcast(FP8X4),
-                rhs_scale=c_scales[i][:],
-                start=True,
-                stop=True,
-            )
-
-        def store(i, c0, n, src, copy):
-            res = keep.tile([P, n, half], F32, name=f"res{i}_{c0}")
+        def store(b, c0, n, src, copy):
+            res = keep.tile([P, n, P], F32, name=f"res{b}_{c0}")
             copy(res[:], src.rearrange("p (c t) -> p c t", c=n))
             nc.sync.dma_start(
-                out=out.rearrange("(c p) t -> p c t", p=P)[:, c0 : c0 + n, i * half : (i + 1) * half],
-                in_=res[:],
+                out=out.rearrange("(c p) t -> p c t", p=P)[:, c0 : c0 + n, b * P : (b + 1) * P], in_=res[:]
             )
 
-        for a in range(0, S, XG):
-            gather_tokens(a)
-        for e in range(whole):
-            piece(320, 0, e, 0, H, bank[e % 2])
+        def turn_gate(bk):
+            line = gate_line[:].rearrange("p r t -> p (r t)")
+            for i in range(4):
+                nc.tensor.transpose(bk[:, i * P : (i + 1) * P], line[:, i * P : (i + 1) * P], ident[:])
+            nc.scalar.copy(gate_cols[:], bk[:, 0:512:P])
+
+        def gated(e, after):
+            sa = silu(e, after)
+            for t in range(PACK):
+                product(e, t, sa, bank[2 + e % 2][:, t * C : (t + 1) * C])
+
+        gather_words(0)
+        gather_bytes(0)
+        for e in range(E - 1):
+            later = e + 1 if e + 1 < S // XG else None
+            multiply(cast(0, e, SCALAR_COLS, f"words{later}" if later else None), e, 0, PACK, bank[e % 2])
+            if later:
+                gather_words(later)
             if e > 0:
-                gate_whole(e - 1, raw[(0, e, 0)][:, 0, :].rearrange("p (q c) -> p q c", c=C))
-            piece(320 if e < whole - 1 else 192, 1, e, 0, H, bank[2 + e % 2])
+                gated(e - 1, (0, e))
             if e == 2:
-                spread_gate()
-        for q in range(CH):
-            split_chunk(q)
-        for q in range(CH - 1):
-            round_sum(0, TB, q, bank[4 + q][:])
-        last_chunk(0)
-        last_chunk(1)
-        turn_back(0)
-        last_chunk(2)
-        turn_back(1)
-        last_chunk(3)
-        turn_back(2)
-        turn_back(3)
-        for c in range(4):
-            project(0, c, bank[(0, 7)[c // 2]][:, (c % 2) * half : (c % 2 + 1) * half])
-        for c in range(4):
-            project(1, c, bank[(3, 6, 2, 4)[c]][:, 0:half])
-        store(0, 0, 2, bank[0][:], nc.scalar.copy)
-        store(0, 2, 2, bank[7][:], nc.vector.tensor_copy)
-        for c in range(4):
-            store(1, c, 1, bank[(3, 6, 2, 4)[c]][:, 0:half], (nc.scalar.copy, nc.vector.tensor_copy)[c % 2])
+                turn_gate(bank[1])
+            multiply(cast(1, e, SCALAR_COLS, f"bytes{later}" if later else None), e, 0, PACK, bank[2 + e % 2])
+            if later:
+                gather_bytes(later)
+        e = E - 1
+        gated(e - 1, (1, e - 1))
+        multiply(cast(0, e, SCALAR_COLS), e, 0, PACK, bank[e % 2])
+        g = cast(1, e, SCALAR_COLS_LAST)
+        sa = silu(e, (1, e))
+        last = [bank[i][:, 0:C] for i in (3, 2, 0, 7)]
+        for t in range(PACK):
+            multiply(g, e, t, 1, last[t])
+        for t in range(PACK):
+            product(e, t, sa, last[t])
+
+        for t in range(PACK):
+            plain_gather(0, 2, 0, t)
+        for t in range(PACK):
+            plain_gather(0, 1, 1, t)
+        scale_first(0)
+        plain_gather(1, 1, 1, 0, on_scalar=False)
+        for t in range(3):
+            for r in range(2):
+                gated_gather(2, 2, r, t)
+        for r in range(2):
+            gated_gather(2, 1, r, 3)
+        add_second(0)
+        add_both(2)
+        plain_gather(1, 1, 1, 1, picked=plain[:, 3, 0, 0:P])
+        plain_gather(1, 1, 1, 2, picked=plain[:, 3, 0, P : 2 * P])
+        plain_gather(1, 1, 1, 3, picked=plain[:, 3, 1, 0:P])
+        scale_first(1)
+        copy_back(0)
+        project(2, quarters(bank[2]))
+        gated_gather(3, 1, 0, 3)
+        add_second(1)
+        project(0, quarters(bank[3]))
+        store(2, 0, 4, bank[2][:], nc.scalar.copy)
+        copy_back(1)
+        gated_gather(3, 1, 1, 3)
+        add_both(3)
+        store(0, 0, 4, bank[3][:], nc.scalar.copy)
+        project(1, quarters(bank[4]))
+        project(3, quarters(bank[5])[0:2] + quarters(bank[0])[0:2])
+        store(1, 0, 4, bank[4][:], nc.scalar.copy)
+        store(3, 0, 2, bank[5][:, 0 : 2 * P], nc.vector.tensor_copy)
+        store(3, 2, 2, bank[0][:, 0 : 2 * P], nc.vector.tensor_copy)

@@ -266,7 +266,6 @@ def tile_moe_sdn_glu_silu_kernel(
         for t in range(PACK):
             plain_gather(0, 1, 1, t)
         scale_first(0)
-        plain_gather(1, 1, 1, 0, on_scalar=False)
         for t in range(3):
             for r in range(2):
                 gated_gather(2, 2, r, t)
@@ -274,6 +273,7 @@ def tile_moe_sdn_glu_silu_kernel(
             gated_gather(2, 1, r, 3)
         add_second(0)
         add_both(2)
+        plain_gather(1, 1, 1, 0)
         plain_gather(1, 1, 1, 1, picked=plain[:, 3, 0, 0:P])
         plain_gather(1, 1, 1, 2, picked=plain[:, 3, 0, P : 2 * P])
         plain_gather(1, 1, 1, 3, picked=plain[:, 3, 1, 0:P])
@@ -288,8 +288,9 @@ def tile_moe_sdn_glu_silu_kernel(
         gated_gather(3, 1, 1, 3)
         add_both(3)
         store(0, 0, 4, bank[3][:], nc.scalar.copy)
-        project(1, quarters(bank[4]))
+        project(1, quarters(bank[4])[0:2] + quarters(bank[6])[0:2])
         project(3, quarters(bank[5])[0:2] + quarters(bank[0])[0:2])
-        store(1, 0, 4, bank[4][:], nc.scalar.copy)
+        store(1, 0, 2, bank[4][:, 0 : 2 * P], nc.vector.tensor_copy)
+        store(1, 2, 2, bank[6][:, 0 : 2 * P], nc.scalar.copy)
         store(3, 0, 2, bank[5][:, 0 : 2 * P], nc.vector.tensor_copy)
-        store(3, 2, 2, bank[0][:, 0 : 2 * P], nc.vector.tensor_copy)
+        store(3, 2, 2, bank[0][:, 0 : 2 * P], nc.scalar.copy)

@@ -38,16 +38,17 @@ def tile_moe_sdn_glu_silu_kernel(
 
         offs_sb = keep.tile([P, S // 16], U16, name="offs_sb")
         pos_sb = [keep.tile([P, T // 16], U16, name=f"pos_sb{r}") for r in range(2)]
-        xw = keep.tile([P, T], I32, name="xw", align_bytes=64)
+        xw = keep.tile([P, T], I32, name="xw", align_bytes=256)
         xs = keep.tile([P, T], U8, name="xs", align_bytes=64)
-        w2w = keep.tile([P, N], I32, name="w2w", align_bytes=64)
+        w2w = keep.tile([P, N], I32, name="w2w", align_bytes=256)
         w2s = keep.tile([P, N], U8, name="w2s", align_bytes=64)
         xgw, xgs = {}, {}
         ident = keep.tile([P, P], F32, name="ident")
         h = [keep.tile([P, S], F32, name=f"h{t}") for t in range(PACK)]
-        gate_rows = keep.tile([P, 2, 2 * P], F32, name="gate_rows")
+        gate_rows = keep.tile([P, 2, 2 * P], F32, name="gate_rows", align_bytes=256)
         gate_line = keep.tile([P, 2, 2 * P], F32, name="gate_line")
         gate_cols = keep.tile([P, 4], F32, name="gate_cols")
+
 
         nc.vector.memset(xs[:].bitcast(I32), 0)
         nc.vector.memset(w2s[:].bitcast(I32), 0)
@@ -67,7 +68,7 @@ def tile_moe_sdn_glu_silu_kernel(
         raw = {}
 
         def load_matrix(m, e):
-            t = keep.tile([P, PACK, H], F32, name=f"raw{m}_{e}")
+            t = keep.tile([P, PACK, H], F32, name=f"raw{m}_{e}", align_bytes=256)
             nc.sync.dma_start(out=t[:], in_=(w1, w3)[m][e].rearrange("(p j) c -> p j c", j=PACK))
             raw[(m, e)] = t
 
@@ -95,8 +96,8 @@ def tile_moe_sdn_glu_silu_kernel(
             nc.vector.tensor_copy(xgs[i][:], xs[:].indirect(offs_sb[:, i * XG // 16 : (i + 1) * XG // 16]))
 
         def quantize(src, width, tag):
-            codes = ring.tile([P, width], U32, name="codes", tag=f"codes{tag}", align_bytes=64, bufs=4)
-            scales = ring.tile([P, width], U8, name="scales", tag=f"scales{tag}", align_bytes=64, bufs=4)
+            codes = ring.tile([P, width], U32, name="codes", tag=f"codes{tag}", align_bytes=64, bufs=8 if width == P else 3)
+            scales = ring.tile([P, width], U8, name="scales", tag=f"scales{tag}", align_bytes=64, bufs=8 if width == P else 3)
             nc.vector.quantize_mx(out=codes[:].bitcast(FP8X4), scales=scales[:], in_=src)
             return codes, scales
 
@@ -219,10 +220,10 @@ def tile_moe_sdn_glu_silu_kernel(
             return [bk[:, c * P : (c + 1) * P] for c in range(4)]
 
         def store(b, c0, n, src, copy):
-            res = keep.tile([P, n, P], F32, name=f"res{b}_{c0}")
-            copy(res[:], src.rearrange("p (c t) -> p c t", c=n))
+            res = raw[(1, b)][:, 1, c0 * P : (c0 + n) * P].rearrange("p (c t) -> p c t", c=n)
+            copy(res, src.rearrange("p (c t) -> p c t", c=n))
             nc.sync.dma_start(
-                out=out.rearrange("(c p) t -> p c t", p=P)[:, c0 : c0 + n, b * P : (b + 1) * P], in_=res[:]
+                out=out.rearrange("(c p) t -> p c t", p=P)[:, c0 : c0 + n, b * P : (b + 1) * P], in_=res
             )
 
         def turn_gate(bk):
@@ -240,19 +241,28 @@ def tile_moe_sdn_glu_silu_kernel(
         gather_bytes(0)
         for e in range(E - 1):
             later = e + 1 if e + 1 < S // XG else None
-            multiply(cast(0, e, SCALAR_COLS, f"words{later}" if later else None), e, 0, PACK, bank[e % 2])
+            share = SCALAR_COLS if e < E - 3 else 208
+            multiply(cast(0, e, share, f"words{later}" if later else None), e, 0, PACK, bank[e % 2])
             if later:
                 gather_words(later)
             if e > 0:
                 gated(e - 1, (0, e))
             if e == 2:
                 turn_gate(bank[1])
-            multiply(cast(1, e, SCALAR_COLS, f"bytes{later}" if later else None), e, 0, PACK, bank[2 + e % 2])
+            if e < E - 2:
+                share = SCALAR_COLS if e < E - 3 else 256
+                multiply(cast(1, e, share, f"bytes{later}" if later else None), e, 0, PACK, bank[2 + e % 2])
             if later:
                 gather_bytes(later)
         e = E - 1
-        gated(e - 1, (1, e - 1))
-        multiply(cast(0, e, SCALAR_COLS), e, 0, PACK, bank[e % 2])
+        g = cast(1, e - 1, 256)
+        early = [bank[4 + t][:, 0:C] for t in range(PACK)]
+        for t in range(PACK):
+            multiply(g, e - 1, t, 1, early[t])
+        sa = silu(e - 1, (1, e - 1))
+        for t in range(PACK):
+            product(e - 1, t, sa, early[t])
+        multiply(cast(0, e, 288), e, 0, PACK, bank[e % 2])
         g = cast(1, e, SCALAR_COLS_LAST)
         sa = silu(e, (1, e))
         last = [bank[i][:, 0:C] for i in (3, 2, 0, 7)]

from contextlib import ExitStack

import concourse.mybir as mybir
from concourse.masks import make_identity

K, T, E, C, H, N = 512, 512, 8, 128, 512, 512
S = E * C
FLOPS = 2 * 2 * K * H * S + 2 * H * N * T

F32 = mybir.dt.float32
BF16 = mybir.dt.bfloat16
I32 = mybir.dt.int32
U32 = mybir.dt.uint32
U16 = mybir.dt.uint16
U8 = mybir.dt.uint8
FP8X4 = mybir.dt.float8_e4m3fn_x4
SILU = mybir.ActivationFunctionType.Silu
COPY = mybir.ActivationFunctionType.Copy
MULT = mybir.AluOpType.mult
ADD = mybir.AluOpType.add

P = 128
PACK = 4
XG = 256
SCALAR_COLS = 288
SCALAR_COLS_LAST = 176


def tile_moe_sdn_glu_silu_kernel(
    tc, x_words, x_scales, w1, w3, w2_words, w2_scales, gate, offs, pos1, pos2, out
):
    nc = tc.nc
    with ExitStack() as ctx:
        keep = ctx.enter_context(tc.tile_pool(name="keep", bufs=1))
        ring = ctx.enter_context(tc.tile_pool(name="ring", bufs=3))
        psum = ctx.enter_context(tc.psum_pool(name="psum", bufs=1))
        bank = [psum.tile([P, 512], F32, name=f"bank{i}") for i in range(8)]

        offs_sb = keep.tile([P, S // 16], U16, name="offs_sb")
        pos_sb = [keep.tile([P, T // 16], U16, name=f"pos_sb{r}") for r in range(2)]
        xw = keep.tile([P, T], I32, name="xw", align_bytes=256)
        xs = keep.tile([P, T], U8, name="xs", align_bytes=64)
        w2w = keep.tile([P, N], I32, name="w2w", align_bytes=256)
        w2s = keep.tile([P, N], U8, name="w2s", align_bytes=64)
        xgw, xgs = {}, {}
        ident = keep.tile([P, P], F32, name="ident")
        h = [keep.tile([P, S], F32, name=f"h{t}") for t in range(PACK)]
        gate_rows = keep.tile([P, 2, 2 * P], F32, name="gate_rows", align_bytes=256)
        gate_line = keep.tile([P, 2, 2 * P], F32, name="gate_line")
        gate_cols = keep.tile([P, 4], F32, name="gate_cols")


        nc.vector.memset(xs[:].bitcast(I32), 0)
        nc.vector.memset(w2s[:].bitcast(I32), 0)
        nc.vector.memset(gate_line[:], 0.0)
        make_identity(nc, ident[:])

        def load_scales(plane, rows):
            for g in range(4):
                nc.sync.dma_start(
                    out=plane[32 * g : 32 * g + 4, :].bitcast(I32),
                    in_=rows[4 * g : 4 * g + 4, :].bitcast(I32),
                )

        def load_words(tile, words):
            nc.sync.dma_start(out=tile[:], in_=words.rearrange("p t d -> p (t d)").bitcast(I32))

        raw = {}

        def load_matrix(m, e):
            t = keep.tile([P, PACK, H], F32, name=f"raw{m}_{e}", align_bytes=256)
            nc.sync.dma_start(out=t[:], in_=(w1, w3)[m][e].rearrange("(p j) c -> p j c", j=PACK))
            raw[(m, e)] = t

        nc.sync.dma_start(offs_sb[:], offs)
        load_words(xw, x_words[0])
        load_matrix(0, 0)
        load_scales(xs, x_scales[0])
        load_matrix(1, 0)
        nc.sync.dma_start(gate_line[0:1], gate[:, 0:1, 0 : 2 * P].rearrange("r p t -> p r t"))
        for e in range(1, E):
            load_matrix(0, e)
            load_matrix(1, e)
        nc.sync.dma_start(pos_sb[0][:], pos1)
        nc.sync.dma_start(pos_sb[1][:], pos2)
        nc.sync.dma_start(gate_rows[:], gate[:, :, 2 * P :].rearrange("r p t -> p r t"))
        load_words(w2w, w2_words[0])
        load_scales(w2s, w2_scales[0])

        def gather_words(i):
            xgw[i] = keep.tile([P, XG], U32, name="xgw", tag=f"words{i}", align_bytes=64)
            nc.vector.tensor_copy(xgw[i][:], xw[:].bitcast(U32).indirect(offs_sb[:, i * XG // 16 : (i + 1) * XG // 16]))

        def gather_bytes(i):
            xgs[i] = keep.tile([P, XG], U8, name="xgs", tag=f"bytes{i}", align_bytes=64)
            nc.vector.tensor_copy(xgs[i][:], xs[:].indirect(offs_sb[:, i * XG // 16 : (i + 1) * XG // 16]))

        def quantize(src, width, tag):
            codes = ring.tile([P, width], U32, name="codes", tag=f"codes{tag}", align_bytes=64, bufs=8 if width == P else 3)
            scales = ring.tile([P, width], U8, name="scales", tag=f"scales{tag}", align_bytes=64, bufs=8 if width == P else 3)
            nc.vector.quantize_mx(out=codes[:].bitcast(FP8X4), scales=scales[:], in_=src)
            return codes, scales

        def cast(m, e, scalar_cols, slot=None):
            if slot is None:
                g = ring.tile([P, PACK, P, PACK], BF16, name="grouped", tag="grouped", align_bytes=64, bufs=4)
            else:
                g = keep.tile([P, PACK, P, PACK], BF16, name="grouped", tag=slot, align_bytes=64)
            src = raw[(m, e)][:].rearrange("p j (m t) -> p m j t", t=PACK)
            dst = g[:].rearrange("p t m j -> p m j t")
            cut = scalar_cols // PACK
            nc.scalar.copy(dst[:, 0:cut], src[:, 0:cut])
            nc.vector.tensor_copy(dst[:, cut:P], src[:, cut:P])
            return g

        def multiply(g, e, t0, nt, acc):
            codes, scales = quantize(g[:, t0 : t0 + nt].rearrange("p t m j -> p (t m j)"), nt * P, f"w{nt}")
            cols = slice((e % 2) * C, (e % 2 + 1) * C)
            for a in range(nt):
                nc.tensor.matmul_mx(
                    out=acc[:, a * C : (a + 1) * C],
                    lhsT=codes[:, a * P : (a + 1) * P].bitcast(FP8X4),
                    lhsT_scale=scales[:, a * P : (a + 1) * P],
                    rhs=xgw[e // 2][:, cols].bitcast(FP8X4),
                    rhs_scale=xgs[e // 2][:, cols],
                    start=True,
                    stop=True,
                )

        def silu(e, after):
            sa = raw[after][:, :, 0:C]
            nc.scalar.activation(sa, bank[e % 2][:].rearrange("p (t c) -> p t c", c=C), SILU)
            return sa

        def product(e, t, sa, acc):
            nc.vector.tensor_tensor(h[t][:, e * C : (e + 1) * C], acc, sa[:, t, :], MULT)

        def offsets(r, t0, n):
            return pos_sb[r][:, t0 // 16 : (t0 + n) // 16]

        plain = raw[(0, 0)][:].rearrange("p t (r c) -> p t r c", r=2)
        direct = keep.tile([P, 22 * P], F32, name="direct", align_bytes=64)
        weighed = [direct[:, a * P : (a + 8) * P].rearrange("p (t c) -> p t c", t=PACK) for a in (0, 11)]

        def turned(b, r):
            return bank[4 + 2 * b + r]

        def plain_gather(b, nb, r, t, on_scalar=True, picked=None):
            if picked is None:
                picked = plain[:, t, r, b * P : (b + nb) * P]
            window = h[t][:].indirect(offsets(r, b * P, nb * P))
            if on_scalar:
                nc.scalar.activation(picked, window, COPY)
            else:
                nc.vector.tensor_copy(picked, window)
            col = P * (t // 2) + 2 * P * (t % 2)
            for a in range(nb):
                nc.tensor.transpose(turned(b + a, r)[:, col : col + P], picked[:, a * P : (a + 1) * P], ident[:])

        def gated_gather(b, nb, r, t):
            cols = slice((b - 2) * P, (b - 2 + nb) * P)
            nc.vector.tensor_tensor(
                weighed[r][:, t, cols], h[t][:].indirect(offsets(r, b * P, nb * P)), gate_rows[:, r, cols], MULT
            )

        first = [direct[:, 7 * P : 11 * P], direct[:, 18 * P : 22 * P]]
        summed = [keep.tile([P, H], BF16, name=f"summed{b}", align_bytes=64) for b in range(2)]
        apart = [keep.tile([P, H], BF16, name=f"apart{b}", align_bytes=64) for b in range(3)]
        cg = [apart[b % 3][:] for b in range(4)]

        def scale_first(b):
            nc.scalar.activation(
                first[b].rearrange("p (w e) -> p w e", e=2),
                turned(b, 0)[:].rearrange("p (e w) -> p w e", e=2),
                COPY,
                scale=gate_cols[:, b : b + 1],
            )

        def add_second(b):
            nc.vector.scalar_tensor_tensor(
                summed[b][:].rearrange("p (w e) -> p w e", e=2),
                turned(b, 1)[:].rearrange("p (e w) -> p w e", e=2),
                gate_cols[:, 2 + b : 3 + b],
                first[b].rearrange("p (w e) -> p w e", e=2),
                MULT,
                ADD,
            )
            words = summed[b][:].bitcast(F32)
            for u in range(2):
                nc.tensor.transpose(bank[b][:, u * P : (u + 1) * P], words[:, u * P : (u + 1) * P], ident[:])

        def copy_back(b):
            nc.scalar.copy(
                cg[b].bitcast(F32).rearrange("p (t u) -> p t u", u=2),
                bank[b][:, 0 : 2 * P].rearrange("p (u t) -> p t u", u=2),
            )

        def add_both(b):
            nc.vector.tensor_tensor(
                cg[b].rearrange("p (c i t) -> p c t i", i=2, t=PACK),
                weighed[0][:, :, (b - 2) * P : (b - 1) * P].rearrange("p t (c i) -> p c t i", i=2),
                weighed[1][:, :, (b - 2) * P : (b - 1) * P].rearrange("p t (c i) -> p c t i", i=2),
                ADD,
            )

        def project(b, accs):
            codes, scales = quantize(cg[b], P, "c")
            for c in range(4):
                nc.tensor.matmul_mx(
                    out=accs[c],
                    lhsT=w2w[:, c * P : (c + 1) * P].bitcast(FP8X4),
                    lhsT_scale=w2s[:, c * P : (c + 1) * P],
                    rhs=codes[:].bitcast(FP8X4),
                    rhs_scale=scales[:],
                    start=True,
                    stop=True,
                )

        def quarters(bk):
            return [bk[:, c * P : (c + 1) * P] for c in range(4)]

        def store(b, c0, n, src, copy):
            res = raw[(1, b)][:, 1, c0 * P : (c0 + n) * P].rearrange("p (c t) -> p c t", c=n)
            copy(res, src.rearrange("p (c t) -> p c t", c=n))
            nc.sync.dma_start(
                out=out.rearrange("(c p) t -> p c t", p=P)[:, c0 : c0 + n, b * P : (b + 1) * P], in_=res
            )

        def turn_gate(bk):
            line = gate_line[:].rearrange("p r t -> p (r t)")
            for i in range(4):
                nc.tensor.transpose(bk[:, i * P : (i + 1) * P], line[:, i * P : (i + 1) * P], ident[:])
            nc.scalar.copy(gate_cols[:], bk[:, 0:512:P])

        def gated(e, after):
            sa = silu(e, after)
            for t in range(PACK):
                product(e, t, sa, bank[2 + e % 2][:, t * C : (t + 1) * C])

        gather_words(0)
        gather_bytes(0)
        for e in range(E - 1):
            later = e + 1 if e + 1 < S // XG else None
            share = SCALAR_COLS if e < E - 3 else 208
            multiply(cast(0, e, share, f"words{later}" if later else None), e, 0, PACK, bank[e % 2])
            if later:
                gather_words(later)
            if e > 0:
                gated(e - 1, (0, e))
            if e == 2:
                turn_gate(bank[1])
            if e < E - 2:
                share = SCALAR_COLS if e < E - 3 else 256
                multiply(cast(1, e, share, f"bytes{later}" if later else None), e, 0, PACK, bank[2 + e % 2])
            if later:
                gather_bytes(later)
        e = E - 1
        g = cast(1, e - 1, 256)
        early = [bank[4 + t][:, 0:C] for t in range(PACK)]
        for t in range(PACK):
            multiply(g, e - 1, t, 1, early[t])
        sa = silu(e - 1, (1, e - 1))
        for t in range(PACK):
            product(e - 1, t, sa, early[t])
        multiply(cast(0, e, 288), e, 0, PACK, bank[e % 2])
        g = cast(1, e, SCALAR_COLS_LAST)
        sa = silu(e, (1, e))
        last = [bank[i][:, 0:C] for i in (3, 2, 0, 7)]
        for t in range(PACK):
            multiply(g, e, t, 1, last[t])
        for t in range(PACK):
            product(e, t, sa, last[t])

        for t in range(PACK):
            plain_gather(0, 2, 0, t)
        for t in range(PACK):
            plain_gather(0, 1, 1, t)
        scale_first(0)
        for t in range(3):
            for r in range(2):
                gated_gather(2, 2, r, t)
        for r in range(2):
            gated_gather(2, 1, r, 3)
        add_second(0)
        add_both(2)
        plain_gather(1, 1, 1, 0)
        plain_gather(1, 1, 1, 1, picked=plain[:, 3, 0, 0:P])
        plain_gather(1, 1, 1, 2, picked=plain[:, 3, 0, P : 2 * P])
        plain_gather(1, 1, 1, 3, picked=plain[:, 3, 1, 0:P])
        scale_first(1)
        copy_back(0)
        project(2, quarters(bank[2]))
        gated_gather(3, 1, 0, 3)
        add_second(1)
        project(0, quarters(bank[3]))
        store(2, 0, 4, bank[2][:], nc.scalar.copy)
        copy_back(1)
        gated_gather(3, 1, 1, 3)
        add_both(3)
        store(0, 0, 4, bank[3][:], nc.scalar.copy)
        project(1, quarters(bank[4])[0:2] + quarters(bank[6])[0:2])
        project(3, quarters(bank[5])[0:2] + quarters(bank[0])[0:2])
        store(1, 0, 2, bank[4][:, 0 : 2 * P], nc.vector.tensor_copy)
        store(1, 2, 2, bank[6][:, 0 : 2 * P], nc.scalar.copy)
        store(3, 0, 2, bank[5][:, 0 : 2 * P], nc.vector.tensor_copy)
        store(3, 2, 2, bank[0][:, 0 : 2 * P], nc.scalar.copy)
